import numpy as np, ml_dtypes
CORES = [13,21,141,149]
N = 4
BF = ml_dtypes.bfloat16
def gentries(a):
    return np.ascontiguousarray(a.reshape(8, 16, -1).transpose(0, 2, 1)).reshape(8, -1)
def gtable(e):
    e = np.asarray(e); return np.ascontiguousarray(e.reshape(8, -1, 16).transpose(0, 2, 1)).reshape(128, -1).astype(np.int32)
S, K, W, C, RO = 256, 16, 2048, 8, 5
def H(e, v):
    return ((e * v >> 5) + e + 37 * v) & (W - 1)
def U(x, w):
    return np.add.reduce(x * w, axis=-1, dtype=np.int32) & (W - 1)
def applies(d, x, least):
    return np.add.reduce(d > x, axis=-1, dtype=np.int32) >= least
def parts(rng):
    lev = rng.choice(np.array([96, 160, 256]), (N, 8, 1, W))
    d = (rng.random((N, 8, 16, W)) * lev).astype(np.int64)
    return d, rng.integers(0, W, (N, 8, S, K)), rng.integers(0, 256, (N, 8, 16, S)), rng.integers(1, 256, (N, 8, 16))
def pack(d, e, z, w):
    return {"dv": d.reshape(N, 128, W).astype(np.float32).astype(BF), "ef": np.stack([gtable(a.reshape(8, -1)) for a in e]),
            "zv": z.reshape(N, 128, S).astype(np.float32).astype(BF), "wt": w.reshape(N, 128, 1).astype(np.int32)}
def stage(rng, d, w, r, g):
    o = rng.permutation(16); w[r, g] = 1; w[r, g, o[:8]] = 255
    m = np.zeros(16, np.int64); m[o[:4]] = 255; m[o[8:12]] = 255
    q = np.zeros(16, np.int64); q[rng.permutation(o[:15])[:9]] = 255
    row = int(o[15]); one = np.zeros(16, np.int64); one[row] = 255
    d[r, g, :, 0] = m; d[r, g, :, W - 1] = q; d[r, g, :, H(W - 1, 255 * 1024 & (W - 1))] = 255
    d[r, g, :, H(0, 255)] = m + one; d[r, g, :, H(W - 1, 255)] = q + one
    return row
def setup_inputs(rng):
    return pack(*parts(rng))
def setup_inputs_corners(rng):
    d, e, z, w = parts(rng); i = np.arange(S); kk = np.arange(K)
    for r in range(N):
        for g in range(8):
            if (r + g) % 2 == 1:
                stage(rng, d, w, r, g)
                few = np.argsort(np.argsort(rng.random((16, 64)), axis=0), axis=0) < np.where(np.arange(64) % 4 == 1, 0, 7)
                d[r, g, :, 16:80] = few * rng.integers(1, 256, (16, 64))
                goal = rng.choice(np.array([0, 1, 2, K - 2, K - 1]), S)[:, None]
                cold = rng.integers(16, 80, (S, K))
                v = np.where((kk < goal) | (goal == 0), cold, np.where(kk == goal, W - 1, e[r, g])); v[:, 0] = 0
                m = i % 4 != 3
                e[r, g] = np.where(m[:, None], v, e[r, g]); z[r, g] = np.where(m, 0, z[r, g])
            else:
                e[r, g, ::4] = e[r, g, ::4, :1]; e[r, g, 1::4] = (W - 1) * rng.integers(0, 2, e[r, g, 1::4].shape)
                z[r, g, :, 5::8] = 255; z[r, g, :, 6::8] = 0
    return pack(d, e, z, w)
def setup_inputs_ends(rng):
    p = rng.choice(np.array([0.0, 0.25, 0.5, 0.75, 0.9, 1.0]), (N, 8, 1, W)); d = 255 * (rng.random((N, 8, 16, W)) < p).astype(np.int64)
    d[..., 2::4] = rng.integers(0, 256, d[..., 2::4].shape)
    p = rng.choice(np.array([0.0, 0.1, 0.3, 0.5, 1.0]), (N, 8, 1, S)); z = 255 * (rng.random((N, 8, 16, S)) < p).astype(np.int64)
    z[..., 2::5] = rng.integers(0, 256, z[..., 2::5].shape)
    e = (W - 1) * rng.integers(0, 2, (N, 8, S, K)); w = np.where(rng.random((N, 8, 16)) < 0.5, 1, 255)
    for r in range(N):
        for g in range(8):
            if r < 2:
                row = stage(rng, d, w, r, g); z[r, g] = 0; z[r, g, row] = 255 * rng.integers(0, 2, S); z[r, g, row, 0] = 255; z[r, g, row, S - 1] = 0
                e[r, g, :, 0] = 0; e[r, g, :, 1:3] = 2 + 4 * rng.integers(0, W // 4, (S, 2)); e[r, g, :, K - 1] = W - 1
            elif (r == N - 1 and g == 7) or (r == N - 2 and g == 6):
                w[r, g] = 255; z[r, g, :, 1] = 255; z[r, g, :, S - 1] = 255; z[r, g, :, 3] = 0
            else:
                w[r, g, 13:15] = 1; w[r, g, 15] = 255
                for j in (1, S - 1):
                    z[r, g, :, j] = 0; z[r, g, 13:, j] = 255; e[r, g, j, 0] = W - 1; e[r, g, j, K - 1] = W - 1
    z[0, 7, :, S - 1] = 255
    return pack(d, e, z, w)
def setup_inputs_full(rng):
    d, e, z, w = parts(rng); i = np.arange(S); kk = np.arange(K); quiet = int(rng.integers(0, N)); turn = int(rng.integers(0, 8))
    for r in range(N):
        for g in range(8):
            kind = (5, 1, 5, 3)[g % 4] if r == quiet else (g + 3 * r + turn) % 8
            if kind == 1:
                o = np.argsort(np.argsort(rng.random((16, S)), axis=0), axis=0)
                z[r, g] = np.where(o < rng.integers(9, 17, S), 255, z[r, g])
            elif kind == 2:
                stage(rng, d, w, r, g)
                few = np.argsort(np.argsort(rng.random((16, 64)), axis=0), axis=0) < np.where(np.arange(64) % 4 == 1, 0, 7)
                d[r, g, :, 16:80] = few * rng.integers(1, 256, (16, 64))
                goal = rng.integers(4, K, S)[:, None]
                v = np.where(kk < goal, rng.integers(16, 80, (S, K)), np.where(kk == goal, W - 1, e[r, g])); v[:, 0] = 0
                m = i % 8 != 5
                e[r, g] = np.where(m[:, None], v, e[r, g]); z[r, g] = np.where(m, 0, z[r, g])
            elif kind == 3 or kind == 6:
                d[r, g] = rng.integers(160, 256, (16, W)); z[r, g] = rng.integers(100, 160, (16, S))
                if kind == 6: d[r, g] = np.where(rng.random(W) < 0.04, rng.integers(0, 100, (16, W)), d[r, g])
            elif kind == 4:
                w[r, g] = 255; half = (rng.permutation(16) < 8)[:, None]
                low = half ^ (rng.random(S) < 0.5)
                z[r, g] = np.where(low, rng.integers(0, 5, (16, S)), rng.integers(251, 256, (16, S)))
                t = rng.random(W); top = np.where(t < 0.3, half, np.where(t < 0.6, ~half, t < 0.85))
                v = np.where(top, rng.integers(251, 256, (16, W)), rng.integers(0, 5, (16, W)))
                d[r, g] = np.where((t >= 0.6) & (t < 0.85), 255, v)
            elif kind == 5:
                e[r, g] = e[r, g, :, :1]
            elif kind == 7:
                w[r, g] = 255; z[r, g] = rng.integers(244, 255, (16, S))
                o = np.argsort(np.argsort(rng.random((16, W)), axis=0), axis=0)
                d[r, g] = np.where((o < rng.integers(8, 17, W)) & (rng.random(W) < 0.6), 255, d[r, g])
    return pack(d, e, z, w)
def setup_inputs_spread(rng):
    d = (np.exp2(8 * rng.random((N, 8, 1, W))) * rng.random((N, 8, 16, W))).astype(np.int64)
    z = (np.exp2(8 * rng.random((N, 8, 1, S))) * rng.random((N, 8, 16, S))).astype(np.int64)
    e = np.minimum((np.exp2((W.bit_length() - 1) * rng.random((N, 8, S, K))) * rng.random((N, 8, S, K))).astype(np.int64), W - 1)
    e = np.where(rng.random((N, 8, S, 1)) < 0.5, W - 1 - e, e)
    w = np.minimum(1 + (np.exp2(8 * rng.random((N, 8, 16))) * rng.random((N, 8, 16))).astype(np.int64), 255)
    return pack(np.minimum(d, 255), e, np.minimum(z, 255), w)
def setup_inputs_ties(rng):
    d, e, z, w = parts(rng)
    d = rng.choice(np.array([0, 0, 100, 252]), (N, 8, 1, W)) + rng.integers(0, 4, d.shape)
    z = rng.choice(np.array([0, 100, 100, 252]), (N, 8, 1, S)) + rng.integers(0, 4, z.shape)
    e[:, :, ::4] = e[:, :, ::4, :1]; e[:, :, 1::4] = rng.choice(np.array([0, 1, W - 2, W - 1]), e[:, :, 1::4].shape)
    e[:, :, 2::4, K // 2:] = e[:, :, 2::4, :K // 2]
    return pack(d, e, z, w)
def check_inputs(d):
    bad = []
    for k, lo, hi in (("dv", 0, 255), ("ef", 0, W - 1), ("zv", 0, 255), ("wt", 1, 255)):
        x = np.asarray(d[k]).astype(np.float32)
        if not np.all((x >= lo) & (x <= hi) & (x == np.floor(x))): bad.append("range of " + k)
    return bad
def reference(dv, ef, zv, wt):
    g2 = np.arange(8)[:, None]; g3 = g2[:, :, None]; kk = np.arange(K - 1)
    D = [np.ascontiguousarray(a.astype(np.float32).astype(np.int32).reshape(8, 16, W).transpose(0, 2, 1)) for a in dv]
    E = [gentries(a).astype(np.int32).reshape(8, S, K) for a in ef]
    z = [np.ascontiguousarray(a.astype(np.float32).astype(np.int32).reshape(8, 16, S).transpose(0, 2, 1)) for a in zv]
    w = wt.astype(np.int32).reshape(N, 8, 1, 1, 16)
    A = [0] * N
    for t in range(RO):
        name = []
        for r in range(N):
            least = 8 + (A[r] & 1); e = E[r]; x = z[r][:, :, None, :]
            n = H(e, U(x, w[r]))
            d = D[r][g3, n]
            a = applies(d, x, least)
            zk = np.where(a[..., None], np.abs(x - d), x); z0 = zk[:, :, :1]
            b = applies(D[r][g3, H(e[:, :, :1], U(zk, w[r]))], zk, least)
            c = applies(D[r][g3, H(e, U(z0, w[r]))], z0, least)
            ok = (b != a[:, :, :1]) & (c == a); ok[:, :, 0] = False
            s = np.argmax(ok, axis=2)
            name.append(np.take_along_axis(n, s[:, :, None], 2)[:, :, 0])
            z[r] = np.take_along_axis(zk, s[:, :, None, None], 2)[:, :, 0]
            E[r] = np.concatenate([np.take_along_axis(e, kk + (kk >= s[:, :, None]), 2), np.zeros((8, S, 1), np.int32)], axis=2)
            A[r] = int(np.count_nonzero(s))
        for r in range(N):
            q = (r - 1 - t % (N - 1)) % N
            E[r][:, :, K - 1] = name[q]
            col = C * np.arange(S) + (name[q] & (C - 1))
            D[r][g2, col] = (D[r][g2, col] + z[q]) >> 1
    return {"yd": np.stack([a.transpose(0, 2, 1).reshape(128, W) for a in D]).astype(np.float32).astype(BF),
            "ye": np.stack([gtable(a.reshape(8, -1)) for a in E]).astype(np.float32),
            "yz": np.stack([a.transpose(0, 2, 1).reshape(128, S) for a in z]).astype(np.float32).astype(BF)}

@@ -1,0 +1,532 @@
+import numpy as np
+from concourse.mybir import AluOpType as A
+from concourse.mybir import AxisListType, ActivationFunctionType as AF
+
+RO = 5
+NS = 8
+NENG = 8
+PAY = 288
+BIG = 2.0 ** 25
+
+SCRATCH = {
+    "D": ("sbuf", [128, 2048], "bfloat16"),
+    "Ea": ("sbuf", [128, 256], "float32"), "Eb": ("sbuf", [128, 256], "float32"),
+    "Za": ("sbuf", [128, 544], "bfloat16"), "Zb": ("sbuf", [128, 544], "bfloat16"),
+    "Z4": ("sbuf", [128, 1024], "bfloat16"),
+    "ZK": ("sbuf", [128, 4096], "bfloat16"),
+    "DF": ("sbuf", [128, 4096], "bfloat16"),
+    "SG": ("sbuf", [128, 4096], "bfloat16"),
+    "CC": ("sbuf", [128, 3840], "bfloat16"),
+    "DG": ("sbuf", [128, 2560], "bfloat16"),
+    "BB": ("sbuf", [128, 3840], "bfloat16"),
+    "N": ("sbuf", [128, 256], "int32"), "P": ("sbuf", [128, 256], "int32"), "off": ("sbuf", [128, 256], "uint16"),
+    "Nc": ("sbuf", [128, 240], "int32"), "Pc": ("sbuf", [128, 240], "int32"), "offc": ("sbuf", [128, 240], "uint16"),
+    "Nb": ("sbuf", [128, 240], "int32"), "Pb": ("sbuf", [128, 240], "int32"), "offb": ("sbuf", [128, 240], "uint16"),
+    "Ui": ("sbuf", [128, 240], "int32"), "Ua": ("sbuf", [128, 240], "int32"), "Ub": ("sbuf", [128, 240], "float32"),
+    "vi": ("sbuf", [128, 16], "int32"), "va": ("sbuf", [128, 16], "int32"), "v": ("sbuf", [128, 16], "float32"),
+    "wi": ("sbuf", [128, 16], "int32"), "wa": ("sbuf", [128, 16], "int32"), "w": ("sbuf", [128, 16], "float32"),
+    "a0c": ("sbuf", [128, 16], "float32"), "o0i": ("sbuf", [128, 16], "int32"), "o0u": ("sbuf", [128, 16], "uint16"),
+    "SIG": ("sbuf", [128, 16], "float32"), "Rk": ("sbuf", [128, 256], "float32"), "Tt": ("sbuf", [128, 240], "bfloat16"),
+    "paS": ("sbuf", [128, 240], "float32"), "mm": ("sbuf", [128, 240], "float32"), "Q1": ("sbuf", [128, 240], "float32"),
+    "Q": ("sbuf", [128, 240], "float32"), "y": ("sbuf", [128, 256], "float32"), "x": ("sbuf", [128, 256], "float32"),
+    "Sc": ("sbuf", [128, 256], "float32"), "Oi": ("sbuf", [128, 16], "int32"), "Oj": ("sbuf", [128, 16], "int32"),
+    "ou": ("sbuf", [128, 16], "uint16"), "Ni": ("sbuf", [128, 16], "int32"), "LH": ("sbuf", [128, 32], "int32"),
+    "NB": ("sbuf", [128, 16], "float32"), "S3": ("sbuf", [128, 16], "float32"), "keep": ("sbuf", [128, 240], "float32"),
+    "dE": ("sbuf", [128, 240], "float32"), "kd": ("sbuf", [128, 240], "float32"), "fl": ("sbuf", [128, 16], "bfloat16"),
+    "As": ("sbuf", [128, 1], "float32"), "Ai": ("sbuf", [128, 1], "int32"), "Aj": ("sbuf", [128, 1], "int32"),
+    "PT": ("sbuf", [128, 2], "float32"),
+    "ci": ("sbuf", [128, 16], "int32"), "cu": ("sbuf", [128, 16], "uint16"), "su": ("sbuf", [128, 256], "int32"),
+    "sh": ("sbuf", [128, 256], "int32"), "e15": ("sbuf", [128, 16], "float32"),
+    "EL": ("sbuf", [128, 256], "int32"), "X": ("sbuf", [128, 512], "float32"), "XT": ("sbuf", [128, 512], "float32"),
+    "YL": ("sbuf", [128, 256], "float32"), "wti": ("sbuf", [128, 1], "int32"), "wf": ("sbuf", [128, 1], "float32"),
+    "O8": ("sbuf", [128, 8], "bfloat16"), "B8a": ("sbuf", [128, 8], "bfloat16"), "B8": ("sbuf", [128, 8], "bfloat16"),
+    "F": ("sbuf", [128, 144], "bfloat16"), "Fh": ("sbuf", [128, 144], "bfloat16"), "Fw": ("sbuf", [128, 144], "bfloat16"),
+    "ON": ("sbuf", [128, 256], "bfloat16"), "ID": ("sbuf", [128, 128], "bfloat16"), "NI": ("sbuf", [128, 128], "bfloat16"),
+    "C8": ("sbuf", [128, 128], "bfloat16"), "C1": ("sbuf", [128, 128], "bfloat16"),
+    "ip": ("sbuf", [128, 32], "int32"), "pm": ("sbuf", [128, 32], "int32"), "p16": ("sbuf", [128, 16], "int32"),
+    "p31": ("sbuf", [128, 16], "int32"), "pmf": ("sbuf", [128, 1], "float32"),
+    "i1": ("sbuf", [128, 32], "int32"), "i2": ("sbuf", [128, 16], "int32"), "i3": ("sbuf", [128, 32], "int32"),
+    "i4": ("sbuf", [128, 16], "int32"), "i5": ("sbuf", [128, 16], "int32"), "i6": ("sbuf", [128, 16], "int32"),
+    "i8": ("sbuf", [128, 16], "int32"), "i9": ("sbuf", [128, 256], "int32"), "i10": ("sbuf", [128, 256], "int32"),
+    "t1": ("sbuf", [128, 32], "int32"), "t2": ("sbuf", [128, 32], "int32"),
+    "cl": ("sbuf", [128, 16], "uint16"), "l1": ("sbuf", [128, 32], "uint16"), "l2": ("sbuf", [128, 16], "uint16"),
+    "l3": ("sbuf", [128, 32], "uint16"), "l4": ("sbuf", [128, 16], "uint16"), "pn": ("sbuf", [128, 16], "uint16"),
+    "p2": ("sbuf", [128, 16], "uint16"), "jb": ("sbuf", [128, 16], "float32"),
+    "cb": ("sbuf", [128, 16], "float32"), "KC": ("sbuf", [128, 256], "float32"),
+    "TH": ("sbuf", [128, 256], "float32"), "RS": ("sbuf", [128, 256], "float32"),
+    "pu": ("psum", [128, 512], "float32"), "pa": ("psum", [128, 512], "float32"), "pU": ("psum", [128, 512], "float32"),
+    "pc": ("psum", [128, 512], "float32"), "pb": ("psum", [128, 512], "float32"),
+    "d0": ("psum", [128, 512], "float32"), "d1": ("psum", [128, 512], "float32"), "d2": ("psum", [128, 512], "float32"),
+}
+for _t in range(RO):
+    SCRATCH["L%d" % _t] = ("sbuf", [128, PAY], "bfloat16")
+    SCRATCH["R%d" % _t] = ("sbuf", [128, PAY], "bfloat16")
+PSUM = [k for k in SCRATCH if SCRATCH[k][0] == "psum"]
+DMAS = ["wt", "zv", "ef", "da", "db", "yda", "ydb", "ye", "yz"]
+SEMAPHORES = (["qv", "qs", "qp", "qg"] + ["dma_" + k for k in DMAS] +
+              ["arr%d" % t for t in range(RO)] + ["rl%d" % t for t in range(RO)] + ["loc%d" % t for t in range(RO)])
+
+
+def target(cores, rank, t):
+    return cores[(rank + 1 + t % 3) % len(cores)]
+
+
+def route(topo, src, dst):
+    if topo.may_write(src, dst):
+        return src
+    cand = [c for c in topo.cores_of(src) if c != src and topo.may_write(c, dst)]
+    same = [c for c in cand if topo.die(c) == topo.die(src)]
+    return (same or cand)[0]
+
+
+def engines(topo, src, dst):
+    e = topo.engines(src, dst)[:NENG]
+    return sum(1 << k for k in e), len(e)
+
+
+def relay_program(g, core, T, topo):
+    used = []
+    for t in range(RO):
+        for r in range(len(T.cores)):
+            src, dst = T.cores[r], target(T.cores, r, t)
+            if src != core and route(topo, src, dst) == core:
+                m, n = engines(topo, core, dst)
+                _, nin = engines(topo, src, core)
+                rid, pid = topo.addr(dst, core)
+                g.wait_ge(T.sem["rl%d" % t], nin)
+                g.remote_dma(T["L%d" % t][:, :], T["R%d" % t][:, :], T.sem["arr%d" % t], T.sem["loc%d" % t], pid, rid, m)
+                used.append((t, n))
+    for t, n in used:
+        g.wait_ge(T.sem["loc%d" % t], n)
+
+
+def rank_program(g, core, T, topo):
+    rank = T.rank_of(core)
+    if rank is None:
+        relay_program(g, core, T, topo)
+        return
+    cores = T.cores
+    eng = {"v": g.vector, "s": g.scalar, "p": g.tensor, "g": g, "y": g.sync}
+    known = {k: {} for k in eng}
+    snap, acc, total = {}, {}, {}
+
+    def wait(q, tok):
+        s, n = tok
+        if known[q].get(s, 0) >= n:
+            return
+        eng[q].wait_ge(T.sem[s], n)
+        for a, b in snap.get(tok, {}).items():
+            if known[q].get(a, 0) < b:
+                known[q][a] = b
+        known[q][s] = n
+
+    def before(q, reads, writes):
+        need = {}
+        for regs, wr in ((reads, False), (writes, True)):
+            for b, lo, hi in regs:
+                ps = b in PSUM
+                for l2, h2, w2, tok, q2 in acc.get(b, []):
+                    if ps:
+                        hit = (q2 != q) or (q != "p" and (wr or w2) and lo < h2 and l2 < hi)
+                    else:
+                        hit = (wr or w2) and lo < h2 and l2 < hi
+                    if hit and need.get(tok[0], 0) < tok[1]:
+                        need[tok[0]] = tok[1]
+        for s in sorted(need):
+            wait(q, (s, need[s]))
+
+    def after(q, reads, writes, tok):
+        snap[tok] = dict(known[q])
+        for b, lo, hi in writes:
+            l = acc.get(b, [])
+            acc[b] = [r for r in l if not (lo <= r[0] and r[1] <= hi and b not in PSUM)] + [(lo, hi, True, tok, q)]
+        for b, lo, hi in reads:
+            l = acc.setdefault(b, [])
+            acc[b] = [r for r in l if not (r[4] == q and not r[2] and lo <= r[0] and r[1] <= hi and r[3][0] == tok[0])] + [(lo, hi, False, tok, q)]
+        for b, lo, hi in list(reads) + list(writes):
+            if b in PSUM:
+                last = {}
+                for r in acc[b]:
+                    last[(r[4], r[2], r[0], r[1])] = r
+                acc[b] = list(last.values())
+
+    def op(q, fn, reads, writes):
+        before(q, reads, writes)
+        s = "q" + q
+        total[s] = total.get(s, 0) + 1
+        fn(eng[q]).then_inc(T.sem[s], 1)
+        after(q, reads, writes, (s, total[s]))
+
+    def dma(q, name, out, in_, reads, writes):
+        before(q, reads, writes)
+        s = "dma_" + name
+        eng[q].dma_start(out, in_).then_inc(T.sem[s], 16)
+        total[s] = 16
+        after(q, reads, writes, (s, 16))
+
+    def ap(v):
+        return T[v[0]][:, v[1]:v[2]] if len(v) == 3 else T[v[0]][:, v[1]:v[2]:v[3]]
+
+    def rg(v):
+        return (v[0], v[1], v[2])
+
+    def opnd(v):
+        if isinstance(v[0], tuple):
+            return ap(v[0]).indirect(ap(v[1])), [rg(v[0]), rg(v[1])]
+        return ap(v), [rg(v)]
+
+    def tt(out, a, b, o):
+        oa, orr = opnd(out)
+        aa, ar = opnd(a)
+        ba, br = opnd(b)
+        op("v", lambda e: e.tensor_tensor(oa, aa, ba, o), ar + br + orr[1:], orr[:1])
+
+    def ts(out, a, s1, o1, s2=None, o2=None):
+        oa, orr = opnd(out)
+        aa, ar = opnd(a)
+        rd = list(ar)
+        sc = []
+        for s in (s1, s2):
+            if isinstance(s, tuple):
+                rd.append(rg(s))
+                sc.append(ap(s))
+            else:
+                sc.append(s)
+        if o2 is None:
+            op("v", lambda e: e.tensor_scalar(oa, aa, sc[0], None, o1), rd, orr[:1])
+        else:
+            op("v", lambda e: e.tensor_scalar(oa, aa, sc[0], sc[1], o1, o2), rd, orr[:1])
+
+    def cp(out, a):
+        oa, orr = opnd(out)
+        aa, ar = opnd(a)
+        op("v", lambda e: e.tensor_copy(oa, aa), ar + orr[1:], orr[:1])
+
+    def fill(out, c):
+        op("v", lambda e: e.memset(ap(out), c), [], [rg(out)])
+
+    def act(out, a, f, bias=None, scale=None):
+        aa, ar = opnd(a)
+        kw = {}
+        rd = list(ar)
+        if bias is not None:
+            kw["bias"] = bias
+        if scale is not None:
+            kw["scale"] = ap(scale)
+            rd.append(rg(scale))
+        op("s", lambda e: e.activation(ap(out), aa, f, **kw), rd, [rg(out)])
+
+    def fold(out, fm, src, lo, hi, extra=None):
+        reads = [(fm, 0, 144), (src, lo, hi)]
+        if extra:
+            reads += [rg(extra[0]), rg(extra[1])]
+
+        def fn(e):
+            if extra:
+                e.matmul(ap(out), ap(extra[0]), ap(extra[1]), True, False)
+            for jl in range(16):
+                r = e.matmul(ap(out), T[fm][:, 15 - jl:143 - jl], T[src][:, lo + jl:hi:16], jl == 0 and not extra, jl == 15)
+            return r
+        op("p", fn, reads, [rg(out)])
+
+    def hlist(P, N, off, lo, hi):
+        return [lambda: ts((N, lo, hi), (P, lo, hi), 5, A.logical_shift_right, 2047, A.bitwise_and),
+                lambda: cp((off, lo, hi), (N, lo, hi))]
+
+    E = ["Ea", "Eb"]
+    Z = ["Za", "Zb"]
+    DALL = ("D", 0, 2048)
+
+    dma("s", "ef", T.EL[:, :], T.ef[:, :], [], [("EL", 0, 256)])
+    dma("y", "wt", T.wti[:, :], T.wt[:, :], [], [("wti", 0, 1)])
+    dma("y", "zv", T[Z[0]][:, 256:512], T.zv[:, :], [], [(Z[0], 256, 512)])
+    dma("s", "da", T.D[:, 1184:2048], T.dv[:, 0:864], [], [("D", 1184, 2048)])
+    dma("y", "db", T.D[:, 0:1184], T.dv[:, 864:2048], [], [("D", 0, 1184)])
+
+    def iota(name, pattern, base, cm):
+        n = SCRATCH[name][1][1]
+        op("g", lambda e: e.iota(T[name][:, :], pattern, base, cm), [], [(name, 0, n)])
+
+    fill(("O8", 0, 8), 1.0)
+    fill(("F", 0, 144), 0.0)
+    fill(("ON", 0, 256), 1.0)
+    iota("ip", [[0, 32]], 0, 1)
+    iota("i1", [[16, 16], [0, 2]], 0, 0)
+    op("g", lambda e: e.affine_select(T.B8a[:, :], T.O8[:, :], [[-16, 8]], A.is_ge, 0.0, 0, 1), [("O8", 0, 8)], [("B8a", 0, 8)])
+    op("g", lambda e: e.affine_select(T.B8[:, :], T.B8a[:, :], [[16, 8]], A.is_ge, 0.0, 15, -1), [("B8a", 0, 8)], [("B8", 0, 8)])
+    iota("i2", [[-1, 16]], 15, 32)
+    iota("i5", [[1, 16]], 240, 16)
+    iota("i6", [[1, 16]], 0, 16)
+    iota("i8", [[16, 16]], 0, 0)
+    op("g", lambda e: e.affine_select(T.ID[:, :], T.ON[:, 0:128], [[-1, 128]], A.is_equal, 0.0, 0, 1), [("ON", 0, 128)], [("ID", 0, 128)])
+    iota("i9", [[16, 16], [256, 16]], 1, 0)
+    iota("i4", [[32, 16]], 0, 0)
+    iota("i3", [[1, 16], [0, 2]], 2288, -16)
+    iota("i10", [[1, 16], [0, 16]], 1, 0)
+
+    ts(("pm", 0, 32), ("ip", 0, 32), 15, A.bitwise_and)
+    ts(("p16", 0, 16), ("ip", 0, 16), 16, A.bitwise_and)
+    tt(("t1", 0, 32), ("pm", 0, 32), ("i1", 0, 32), A.add)
+    cp(("cl", 0, 16), ("pm", 0, 16))
+    cp(("l1", 0, 32), ("t1", 0, 32))
+    cp(("F", 15, 128, 16), ("B8", 0, 8))
+    ts(("t2", 0, 16), ("i2", 0, 16), 511, A.bitwise_and)
+    cp(("wf", 0, 1), ("wti", 0, 1))
+    tt(("t2", 16, 32), ("t2", 0, 16), ("p16", 0, 16), A.add)
+    ts(("Fw", 0, 144), ("F", 0, 144), ("wf", 0, 1), A.mult)
+    cp(("l2", 0, 16), ("t2", 16, 32))
+
+    ts(("X", 0, 512), (("EL", 0, 256), ("l1", 0, 32)), 1184.0, A.add)
+    fold(("pu", 0, 16), "Fw", Z[0], 256, 512)
+    cp(("vi", 0, 16), ("pu", 0, 16))
+    op("v", lambda e: e.transpose(T.XT[:, :], T.X[:, :]), [("X", 0, 512)], [("XT", 0, 512)])
+    ts(("va", 0, 16), ("vi", 0, 16), 2047, A.bitwise_and)
+    cp((E[0], 0, 256), (("XT", 0, 512), ("l2", 0, 16)))
+    ts(("v", 0, 16), ("va", 0, 16), 32.0, A.add)
+    tt(("P", 0, 256), (("v", 0, 16), ("cl", 0, 16)), (E[0], 0, 256), A.mult)
+    h = hlist("P", "N", "off", 0, 256)
+    h[0]()
+    ts(("Fh", 0, 144), ("F", 0, 144), 0.5, A.mult)
+    h[1]()
+
+    fill(("PT", 0, 1), 0.0)
+    fill(("PT", 1, 2), 7.5)
+    tt(("jb", 0, 16), ("pm", 0, 16), ("i8", 0, 16), A.add)
+    ts(("NI", 0, 128), ("ID", 0, 128), -1.0, A.mult)
+    cp(("pmf", 0, 1), ("pm", 0, 1))
+    fill(("C8", 0, 128), -1.0 / 16)
+    fill(("C1", 0, 128), -1.0 / 128)
+    ts(("t1", 0, 16), ("i5", 0, 16), 255, A.bitwise_and)
+    ts(("t1", 16, 32), ("i6", 0, 16), 255, A.bitwise_and)
+    ts(("KC", 0, 256), ("i9", 0, 256), ("pmf", 0, 1), A.add, 2048.0, A.mult)
+    cp(("pn", 0, 16), ("t1", 0, 16))
+    cp(("p2", 0, 16), ("t1", 16, 32))
+    ts(("KC", 0, 256), ("KC", 0, 256), -1184.0, A.add)
+    fill(("y", 0, 16), BIG)
+    fill(("RS", 0, 256), 1.0)
+    fill(("RS", 0, 256, 16), 0.0)
+
+    def consts2():
+        ts(("TH", 0, 256), ("i10", 0, 256), 524288.0, A.mult, 864.0, A.add)
+        ts(("ci", 0, 16), ("jb", 0, 16), 148.0, A.add)
+        ts(("p31", 0, 16), ("ip", 0, 16), 31, A.bitwise_and)
+        ts(("t1", 0, 16), ("ci", 0, 16), 255, A.bitwise_and)
+        ts(("t2", 0, 32), ("i3", 0, 32), 255, A.bitwise_and)
+        ts(("cb", 0, 16), ("t1", 0, 16), 8.0, A.mult)
+        tt(("t1", 16, 32), ("p31", 0, 16), ("i4", 0, 16), A.add)
+        cp(("l3", 0, 32), ("t2", 0, 32))
+        cp(("l4", 0, 16), ("t1", 16, 32))
+
+    def z4(src):
+        act(("Z4", 0, 256), src, AF.Copy)
+        act(("Z4", 256, 512), src, AF.Copy)
+        act(("Z4", 512, 1024), ("Z4", 0, 512), AF.Copy)
+
+    z4((Z[0], 256, 512))
+
+    for t in range(RO):
+        ec, en, zc, zn = E[t % 2], E[(t + 1) % 2], Z[t % 2], Z[(t + 1) % 2]
+
+        def g1(lo, hi=None):
+            hi = hi or lo + 1
+            tt(("DF", 256 * lo, 256 * hi), (DALL, ("off", 16 * lo, 16 * hi)), ("Z4", 0, 256 * (hi - lo)), A.subtract)
+
+        def absq(lo, hi):
+            act(("ZK", 256 * lo + 256, 256 * hi + 256), ("DF", 256 * lo, 256 * hi), AF.Abs)
+            fold(("pU", 16 * lo, 16 * hi), "Fw", "ZK", 256 * lo + 256, 256 * hi + 256)
+
+        def sgn(lo, hi):
+            act(("SG", 256 * lo, 256 * hi), ("DF", 256 * lo, 256 * hi), AF.Sign, -0.5)
+
+        def cnta(lo, hi):
+            fold(("pa", 16 * lo, 16 * hi), "Fh", "SG", 256 * lo, 256 * hi)
+
+        g1(15)
+        sgn(15, 16)
+        act((zc, 0, 256), ("DF", 3840, 4096), AF.Abs)
+        fold(("pu", 32, 48), "Fh", "SG", 3840, 4096)
+        act(("Tt", 0, 240), ("ON", 0, 240), AF.Copy, None, ("PT", 1, 2))
+        g1(11, 15)
+        absq(11, 15)
+        ts(("a0c", 0, 16), ("pu", 32, 48), ("PT", 0, 1), A.is_lt, 256.0, A.mult)
+        sgn(11, 15)
+        cnta(11, 15)
+        g1(10)
+        tt(("o0i", 0, 16), ("a0c", 0, 16), ("jb", 0, 16), A.add)
+        g1(9)
+        cp(("o0u", 0, 16), ("o0i", 0, 16))
+        ts(("SIG", 0, 16), ("a0c", 0, 16), 1.0 / 128, A.mult, -1.0, A.add)
+        g1(8)
+        cp(("ZK", 0, 256), ((zc, 0, 512), ("o0u", 0, 16)))
+        fold(("pu", 64, 80), "Fw", "ZK", 0, 256)
+        absq(8, 11)
+        g1(4, 8)
+        absq(4, 8)
+        cp(("wi", 0, 16), ("pu", 64, 80))
+        g1(3)
+        ts(("wa", 0, 16), ("wi", 0, 16), 2047, A.bitwise_and)
+        g1(2)
+        ts(("w", 0, 16), ("wa", 0, 16), 32.0, A.add)
+        g1(1)
+        tt(("Pc", 0, 240), (("w", 0, 16), ("cl", 0, 15)), (ec, 0, 240), A.mult)
+        h = hlist("Pc", "Nc", "offc", 0, 240)
+        g1(0)
+        absq(0, 4)
+        h[0]()
+        tt(("Rk", 0, 256), (("N", 0, 256), ("pn", 0, 16)), ("KC", 0, 256), A.add)
+        h[1]()
+
+        def cv(q):
+            tt(("CC", 256 * q, 256 * q + 256), (DALL, ("offc", 16 * q, 16 * q + 16)), ("ZK", 0, 256), A.is_gt)
+
+        pairs = [(q, min(q + 2, NS)) for q in range(0, NS, 2)]
+
+        def sgath(n):
+            lo, hi = pairs[n]
+            act(("DG", 256 * lo, 256 * hi), (DALL, ("offc", 16 * lo, 16 * hi)), AF.Copy)
+            bank = "d%d" % (n % 3)
+
+            def fn(e):
+                for k in range(hi - lo):
+                    o = ap((bank, 256 * k, 256 * k + 256))
+                    e.matmul(o, T.NI[:, :], T.ZK[:, 0:256], True, False)
+                    r = e.matmul(o, T.ID[:, :], T.DG[:, 256 * (lo + k):256 * (lo + k) + 256], False, True)
+                return r
+            op("p", fn, [("NI", 0, 128), ("ID", 0, 128), ("ZK", 0, 256), ("DG", 256 * lo, 256 * hi)], [(bank, 0, 256 * (hi - lo))])
+
+        def ssign(n):
+            lo, hi = pairs[n]
+            act(("CC", 256 * lo, 256 * hi), ("d%d" % (n % 3), 0, 256 * (hi - lo)), AF.Sign, -0.5)
+
+        vq = list(range(14, NS - 1, -1))
+        chain = [lambda: cp(("Ui", 0, 240), ("pU", 0, 240)),
+                 lambda: ts(("Ua", 0, 240), ("Ui", 0, 240), 2047, A.bitwise_and),
+                 lambda: ts(("Ub", 0, 240), ("Ua", 0, 240), 32.0, A.add),
+                 lambda: tt(("Pb", 0, 240), ((ec, 240, 256), ("cl", 0, 15)), ("Ub", 0, 240), A.mult)]
+        half = len(pairs) // 2
+        for n in range(half):
+            sgath(n)
+            if n:
+                ssign(n - 1)
+        for n, q in enumerate(vq):
+            cv(q)
+            if len(vq) - n <= len(chain):
+                chain[len(chain) - (len(vq) - n)]()
+        fold(("pc", 16 * NS, 240), "F", "CC", 256 * NS, 3840, (("C8", 0, 128), ("ON", 0, 240 - 16 * NS)))
+        for n in range(half, len(pairs)):
+            sgath(n)
+            ssign(n - 1)
+        sgn(8, 11)
+        ssign(len(pairs) - 1)
+        cnta(8, 11)
+        fold(("pc", 0, 16 * NS), "Fh", "CC", 0, 256 * NS)
+        h = hlist("Pb", "Nb", "offb", 0, 240)
+        h[0]()
+        h[1]()
+
+        def bv(lo, hi):
+            tt(("BB", 256 * lo, 256 * hi), (DALL, ("offb", 16 * lo, 16 * hi)), ("ZK", 256 * lo + 256, 256 * hi + 256), A.is_gt)
+            fold(("pb", 16 * lo, 16 * hi), "F", "BB", 256 * lo, 256 * hi, (("C1", 0, 128), ("Tt", 0, 16 * (hi - lo))))
+
+        bv(0, 4)
+        sgn(0, 8)
+        cnta(0, 8)
+        act(("paS", 0, 240), ("pa", 0, 240), AF.Copy)
+        bv(4, 8)
+        bv(8, 12)
+        bv(12, 15)
+        tt(("dE", 0, 240), (ec, 16, 256), (ec, 0, 240), A.subtract)
+        tt(("mm", 0, 240), ("pc", 0, 240), ("paS", 0, 240), A.min)
+        ts(("Q1", 0, 240), ("mm", 0, 240), ("PT", 0, 1), A.is_ge, BIG, A.mult)
+        tt(("Q", 0, 240), (("SIG", 0, 16), ("cl", 0, 15)), ("Q1", 0, 240), A.mult)
+
+        tt(("y", 16, 256), ("pb", 0, 240), ("Q", 0, 240), A.mult)
+        tt(("x", 0, 256), (("y", 0, 256), ("p2", 0, 16)), ("Rk", 0, 256), A.min)
+        op("v", lambda e: e.tensor_tensor_scan(T.Sc[:, :], T.RS[:, :], T.x[:, :], 0.0, A.mult, A.max),
+           [("RS", 0, 256), ("x", 0, 256)], [("Sc", 0, 256)])
+        sv = ("Sc", 15, 256, 16)
+        ts(("Oi", 0, 16), sv, -864.0, A.add)
+        cp(("Ni", 0, 16), sv)
+        ts(("Oj", 0, 16), ("Oi", 0, 16), 11, A.logical_shift_right)
+        ts(("LH", 0, 16), ("Ni", 0, 16), 7, A.bitwise_and)
+        cp(("ou", 0, 16), ("Oj", 0, 16))
+        ts(("LH", 16, 32), ("Ni", 0, 16), 3, A.logical_shift_right, 255, A.bitwise_and)
+        cp((zn, 256, 512), (("ZK", 0, 4096), ("ou", 0, 16)))
+        cp((zn, 512, 544), ("LH", 0, 32))
+
+        dst = target(cores, rank, t)
+        via = route(topo, core, dst)
+        to = dst if via == core else via
+        m, n = engines(topo, core, to)
+        rid, pid = topo.addr(to, core)
+        land, sem = (("L%d" % t), "arr%d" % t) if to == dst else (("R%d" % t), "rl%d" % t)
+        before("g", [(zn, 256, 544)], [])
+        g.remote_dma(T[land][:, :], T[zn][:, 256:544], T.sem[sem], T.sem["loc%d" % t], pid, rid, m)
+        after("g", [(zn, 256, 544)], [], ("loc%d" % t, n))
+        total["loc%d" % t] = n
+        frm = cores[(rank - 1 - t % 3) % len(cores)]
+        lc = "L%d" % t
+        narr = engines(topo, route(topo, frm, core), core)[1]
+        acc[lc] = [(0, PAY, True, ("arr%d" % t, narr), "net")]
+
+        last = t == RO - 1
+        if last:
+            dma("y", "yz", T.yz[:, :], T[zn][:, 256:512], [(zn, 256, 512)], [])
+        else:
+            fold(("pu", 0, 16), "Fw", zn, 256, 512)
+            z4((zn, 256, 512))
+        if t == 0:
+            consts2()
+        ts(("NB", 0, 16), sv, 525152.0, A.is_lt, 67108864.0, A.mult)
+        if not last:
+            ts(("fl", 0, 16), sv, 525152.0, A.is_ge)
+            op("p", lambda e: e.matmul(T.pu[:, 96:112], T.ON[:, 0:128], T.fl[:, :], True, True),
+               [("ON", 0, 128), ("fl", 0, 16)], [("pu", 96, 112)])
+        tt(("S3", 0, 16), sv, ("NB", 0, 16), A.add)
+        tt(("keep", 0, 240), (("S3", 0, 16), ("cl", 0, 15)), ("TH", 16, 256), A.is_lt)
+        if not last:
+            cp(("vi", 0, 16), ("pu", 0, 16))
+        tt(("kd", 0, 240), ("keep", 0, 240), ("dE", 0, 240), A.mult)
+        if not last:
+            ts(("va", 0, 16), ("vi", 0, 16), 2047, A.bitwise_and)
+        tt((en, 16, 256), ("kd", 0, 240), (ec, 0, 240), A.add)
+        if not last:
+            ts(("v", 0, 16), ("va", 0, 16), 32.0, A.add)
+            op("v", lambda e: e.tensor_reduce(T.As[:, :], T.pu[:, 96:112], AxisListType.X, A.add), [("pu", 96, 112)], [("As", 0, 1)])
+            tt(("P", 16, 256), (("v", 0, 16), ("cl", 0, 15)), (en, 16, 256), A.mult)
+            cp(("Ai", 0, 1), ("As", 0, 1))
+            h = hlist("P", "N", "off", 16, 256)
+            h[0]()
+            ts(("Aj", 0, 1), ("Ai", 0, 1), 1, A.bitwise_and)
+            h[1]()
+            cp(("PT", 0, 1), ("Aj", 0, 1))
+            ts(("PT", 1, 2), ("Aj", 0, 1), 7.5, A.add)
+        else:
+            cp(("X", 0, 512), ((en, 0, 256), ("l3", 0, 32)))
+
+        tt(("ci", 0, 16), (lc, 256, 272), ("cb", 0, 16), A.add)
+        ts(("e15", 0, 16), (lc, 272, 288), 8.0, A.mult, 1184.0, A.add)
+        cp(("cu", 0, 16), ("ci", 0, 16))
+        tt((en, 0, 16), ("e15", 0, 16), (lc, 256, 272), A.add)
+        tt(("su", 0, 256), (DALL, ("cu", 0, 16)), (lc, 0, 256), A.add)
+        if not last:
+            tt(("P", 0, 16), ("v", 0, 16), (en, 0, 16), A.mult)
+        ts(("sh", 0, 256), ("su", 0, 256), 1, A.logical_shift_right)
+        if not last:
+            h = hlist("P", "N", "off", 0, 16)
+            h[0]()
+        cp((DALL, ("cu", 0, 16)), ("sh", 0, 256))
+        if not last:
+            h[1]()
+            continue
+
+        dma("y", "yda", T.yd[:, 864:2048], T.D[:, 0:1184], [("D", 0, 1184)], [])
+        dma("s", "ydb", T.yd[:, 0:864], T.D[:, 1184:2048], [("D", 1184, 2048)], [])
+        cp(("X", 15, 512, 32), (en, 0, 16))
+        cp(("X", 31, 512, 32), (en, 0, 16))
+        op("v", lambda e: e.transpose(T.XT[:, :], T.X[:, :]), [("X", 0, 512)], [("XT", 0, 512)])
+        ts(("YL", 0, 256), (("XT", 0, 512), ("l4", 0, 16)), -1184.0, A.add)
+        dma("y", "ye", T.ye[:, :], T.YL[:, :], [("YL", 0, 256)], [])
+
+    for s in sorted(total):
+        wait("g", (s, total[s]))

@@ -1,67 +1,52 @@
 import numpy as np
 from concourse.mybir import AluOpType as A
-from concourse.mybir import AxisListType, ActivationFunctionType as AF
+from concourse.mybir import ActivationFunctionType as AF
 
 RO = 5
 NS = 8
 NENG = 8
 PAY = 288
 BIG = 2.0 ** 25
+FLOOR = -1055.5 / 2048
+
+
+def _s(n, dt):
+    return ("sbuf", [128, n], dt)
+
 
 SCRATCH = {
-    "D": ("sbuf", [128, 2048], "bfloat16"),
-    "Ea": ("sbuf", [128, 256], "float32"), "Eb": ("sbuf", [128, 256], "float32"),
-    "Za": ("sbuf", [128, 544], "bfloat16"), "Zb": ("sbuf", [128, 544], "bfloat16"),
-    "Z4": ("sbuf", [128, 1024], "bfloat16"),
-    "ZK": ("sbuf", [128, 4096], "bfloat16"),
-    "DF": ("sbuf", [128, 4096], "bfloat16"),
-    "SG": ("sbuf", [128, 4096], "bfloat16"),
-    "CC": ("sbuf", [128, 3840], "bfloat16"),
-    "DG": ("sbuf", [128, 2560], "bfloat16"),
-    "BB": ("sbuf", [128, 3840], "bfloat16"),
-    "N": ("sbuf", [128, 256], "int32"), "P": ("sbuf", [128, 256], "int32"), "off": ("sbuf", [128, 256], "uint16"),
-    "Nc": ("sbuf", [128, 240], "int32"), "Pc": ("sbuf", [128, 240], "int32"), "offc": ("sbuf", [128, 240], "uint16"),
-    "Nb": ("sbuf", [128, 240], "int32"), "Pb": ("sbuf", [128, 240], "int32"), "offb": ("sbuf", [128, 240], "uint16"),
-    "Ui": ("sbuf", [128, 240], "int32"), "Ua": ("sbuf", [128, 240], "int32"), "Ub": ("sbuf", [128, 240], "float32"),
-    "vi": ("sbuf", [128, 16], "int32"), "va": ("sbuf", [128, 16], "int32"), "v": ("sbuf", [128, 16], "float32"),
-    "wi": ("sbuf", [128, 16], "int32"), "wa": ("sbuf", [128, 16], "int32"), "w": ("sbuf", [128, 16], "float32"),
-    "a0c": ("sbuf", [128, 16], "float32"), "o0i": ("sbuf", [128, 16], "int32"), "o0u": ("sbuf", [128, 16], "uint16"),
-    "SIG": ("sbuf", [128, 16], "float32"), "Rk": ("sbuf", [128, 256], "float32"), "Tt": ("sbuf", [128, 240], "bfloat16"),
-    "paS": ("sbuf", [128, 240], "float32"), "mm": ("sbuf", [128, 240], "float32"), "Q1": ("sbuf", [128, 240], "float32"),
-    "Q": ("sbuf", [128, 240], "float32"), "y": ("sbuf", [128, 256], "float32"), "x": ("sbuf", [128, 256], "float32"),
-    "Sc": ("sbuf", [128, 256], "float32"), "Oi": ("sbuf", [128, 16], "int32"), "Oj": ("sbuf", [128, 16], "int32"),
-    "ou": ("sbuf", [128, 16], "uint16"), "Ni": ("sbuf", [128, 16], "int32"), "LH": ("sbuf", [128, 32], "int32"),
-    "NB": ("sbuf", [128, 16], "float32"), "S3": ("sbuf", [128, 16], "float32"), "keep": ("sbuf", [128, 240], "float32"),
-    "dE": ("sbuf", [128, 240], "float32"), "kd": ("sbuf", [128, 240], "float32"), "fl": ("sbuf", [128, 16], "bfloat16"),
-    "As": ("sbuf", [128, 1], "float32"), "Ai": ("sbuf", [128, 1], "int32"), "Aj": ("sbuf", [128, 1], "int32"),
-    "PT": ("sbuf", [128, 2], "float32"),
-    "ci": ("sbuf", [128, 16], "int32"), "cu": ("sbuf", [128, 16], "uint16"), "su": ("sbuf", [128, 256], "int32"),
-    "sh": ("sbuf", [128, 256], "int32"), "e15": ("sbuf", [128, 16], "float32"),
-    "EL": ("sbuf", [128, 256], "int32"), "X": ("sbuf", [128, 512], "float32"), "XT": ("sbuf", [128, 512], "float32"),
-    "YL": ("sbuf", [128, 256], "float32"), "wti": ("sbuf", [128, 1], "int32"), "wf": ("sbuf", [128, 1], "float32"),
-    "O8": ("sbuf", [128, 8], "bfloat16"), "B8a": ("sbuf", [128, 8], "bfloat16"), "B8": ("sbuf", [128, 8], "bfloat16"),
-    "F": ("sbuf", [128, 144], "bfloat16"), "Fh": ("sbuf", [128, 144], "bfloat16"), "Fw": ("sbuf", [128, 144], "bfloat16"),
-    "ON": ("sbuf", [128, 256], "bfloat16"), "ID": ("sbuf", [128, 128], "bfloat16"), "NI": ("sbuf", [128, 128], "bfloat16"),
-    "C8": ("sbuf", [128, 128], "bfloat16"), "C1": ("sbuf", [128, 128], "bfloat16"),
-    "ip": ("sbuf", [128, 32], "int32"), "pm": ("sbuf", [128, 32], "int32"), "p16": ("sbuf", [128, 16], "int32"),
-    "p31": ("sbuf", [128, 16], "int32"), "pmf": ("sbuf", [128, 1], "float32"),
-    "i1": ("sbuf", [128, 32], "int32"), "i2": ("sbuf", [128, 16], "int32"), "i3": ("sbuf", [128, 32], "int32"),
-    "i4": ("sbuf", [128, 16], "int32"), "i5": ("sbuf", [128, 16], "int32"), "i6": ("sbuf", [128, 16], "int32"),
-    "i8": ("sbuf", [128, 16], "int32"), "i9": ("sbuf", [128, 256], "int32"), "i10": ("sbuf", [128, 256], "int32"),
-    "t1": ("sbuf", [128, 32], "int32"), "t2": ("sbuf", [128, 32], "int32"),
-    "cl": ("sbuf", [128, 16], "uint16"), "l1": ("sbuf", [128, 32], "uint16"), "l2": ("sbuf", [128, 16], "uint16"),
-    "l3": ("sbuf", [128, 32], "uint16"), "l4": ("sbuf", [128, 16], "uint16"), "pn": ("sbuf", [128, 16], "uint16"),
-    "p2": ("sbuf", [128, 16], "uint16"), "jb": ("sbuf", [128, 16], "float32"),
-    "cb": ("sbuf", [128, 16], "float32"), "KC": ("sbuf", [128, 256], "float32"),
-    "TH": ("sbuf", [128, 256], "float32"), "RS": ("sbuf", [128, 256], "float32"),
-    "pu": ("psum", [128, 512], "float32"), "pa": ("psum", [128, 512], "float32"), "pU": ("psum", [128, 512], "float32"),
-    "pc": ("psum", [128, 512], "float32"), "pb": ("psum", [128, 512], "float32"),
-    "d0": ("psum", [128, 512], "float32"), "d1": ("psum", [128, 512], "float32"), "d2": ("psum", [128, 512], "float32"),
+    "Ea": _s(256, "float32"), "Eb": _s(256, "float32"),
+    "Za": _s(544, "bfloat16"), "Zb": _s(544, "bfloat16"),
 }
+for _n, _w in (("D", 2048), ("Z4", 1024),
+               ("ZK", 4096),
+               ("DF", 4096), ("SG", 4096),
+               ("CC", 3840), ("BB", 3840),
+               ("DG", 256 * NS),
+               ("Tt", 240), ("Th", 240),
+               ("fl", 16), ("O8", 8), ("B8a", 8), ("B8", 8), ("F", 144), ("Fh", 144), ("Fw", 144), ("FB", 144), ("FhB", 144),
+               ("ON", 256), ("ID", 128), ("NI", 128), ("C1", 128), ("CB", 128), ("C32", 128)):
+    SCRATCH[_n] = _s(_w, "bfloat16")
+for _n, _w in (("v", 16), ("w", 16), ("Ub", 240), ("a0c", 16), ("SB", 240), ("Rk", 256), ("Rg", 256), ("pcS", 240), ("mm", 256),
+               ("y", 256), ("x", 256), ("Sc", 256), ("NB", 16), ("S3", 16), ("keep", 240), ("kd", 240), ("As", 1), ("jk", 16),
+               ("PT", 3),
+               ("e15", 16), ("e16", 16), ("X", 512), ("XT", 512), ("YL", 256), ("wf", 1), ("IF", 128), ("JF", 128), ("pmf", 1),
+               ("jb", 16), ("cb", 16), ("KC", 256), ("TH", 256), ("RS", 256)):
+    SCRATCH[_n] = _s(_w, "float32")
+for _n, _w in (("N", 256), ("P", 256), ("Nc", 240), ("Pc", 240), ("Nb", 240), ("Pb", 240), ("Ui", 240), ("vi", 16), ("wi", 16),
+               ("o0i", 16), ("Oj", 16), ("Ni", 16), ("LH", 32), ("Ai", 1), ("Aj", 1), ("ci", 16), ("su", 256), ("sh", 256),
+               ("EL", 256), ("wti", 1), ("ip", 32), ("pm", 32), ("p16", 16), ("p31", 16), ("i1", 32), ("i2", 16), ("i3", 32),
+               ("i4", 16), ("i5", 16), ("i6", 16), ("i8", 16), ("i9", 256), ("i10", 256), ("t1", 32), ("t2", 32)):
+    SCRATCH[_n] = _s(_w, "int32")
+for _n, _w in (("off", 256), ("offc", 240), ("offb", 240), ("o0u", 16), ("ou", 16), ("cu", 16), ("cl", 16), ("l1", 32),
+               ("l2", 16), ("l3", 32), ("l4", 16), ("pn", 16), ("p2", 16)):
+    SCRATCH[_n] = _s(_w, "uint16")
+PSUM = ["pu", "pa", "pU", "pc", "pb", "d0", "d1", "d2"]
+for _n in PSUM:
+    SCRATCH[_n] = ("psum", [128, 512], "float32")
 for _t in range(RO):
-    SCRATCH["L%d" % _t] = ("sbuf", [128, PAY], "bfloat16")
-    SCRATCH["R%d" % _t] = ("sbuf", [128, PAY], "bfloat16")
-PSUM = [k for k in SCRATCH if SCRATCH[k][0] == "psum"]
+    SCRATCH["L%d" % _t] = _s(PAY, "bfloat16")
+    SCRATCH["R%d" % _t] = _s(PAY, "bfloat16")
 DMAS = ["wt", "zv", "ef", "da", "db", "yda", "ydb", "ye", "yz"]
 SEMAPHORES = (["qv", "qs", "qp", "qg"] + ["dma_" + k for k in DMAS] +
               ["arr%d" % t for t in range(RO)] + ["rl%d" % t for t in range(RO)] + ["loc%d" % t for t in range(RO)])
@@ -209,25 +194,29 @@ def rank_program(g, core, T, topo):
         aa, ar = opnd(a)
         kw = {}
         rd = list(ar)
-        if bias is not None:
-            kw["bias"] = bias
-        if scale is not None:
-            kw["scale"] = ap(scale)
-            rd.append(rg(scale))
+        for k, c in (("bias", bias), ("scale", scale)):
+            if isinstance(c, tuple):
+                kw[k] = ap(c)
+                rd.append(rg(c))
+            elif c is not None:
+                kw[k] = c
         op("s", lambda e: e.activation(ap(out), aa, f, **kw), rd, [rg(out)])
 
-    def fold(out, fm, src, lo, hi, extra=None):
+    def fold(out, fm, src, lo, hi, *extra):
         reads = [(fm, 0, 144), (src, lo, hi)]
-        if extra:
-            reads += [rg(extra[0]), rg(extra[1])]
+        for x in extra:
+            reads += [rg(x[0]), rg(x[1])]
 
         def fn(e):
-            if extra:
-                e.matmul(ap(out), ap(extra[0]), ap(extra[1]), True, False)
+            for x in extra:
+                e.matmul(ap(out), ap(x[0]), ap(x[1]), x is extra[0], False)
             for jl in range(16):
                 r = e.matmul(ap(out), T[fm][:, 15 - jl:143 - jl], T[src][:, lo + jl:hi:16], jl == 0 and not extra, jl == 15)
             return r
         op("p", fn, reads, [rg(out)])
+
+    def usum(bank, lo, hi, src, slo, shi):
+        fold((bank, lo, hi), "Fw", src, slo, shi, (("C32", 0, 128), ("ON", 0, hi - lo)))
 
     def hlist(P, N, off, lo, hi):
         return [lambda: ts((N, lo, hi), (P, lo, hi), 5, A.logical_shift_right, 2047, A.bitwise_and),
@@ -259,7 +248,7 @@ def rank_program(g, core, T, topo):
     iota("i6", [[1, 16]], 0, 16)
     iota("i8", [[16, 16]], 0, 0)
     op("g", lambda e: e.affine_select(T.ID[:, :], T.ON[:, 0:128], [[-1, 128]], A.is_equal, 0.0, 0, 1), [("ON", 0, 128)], [("ID", 0, 128)])
-    iota("i9", [[16, 16], [256, 16]], 1, 0)
+    iota("i9", [[16, 16], [256, 16]], 0, 0)
     iota("i4", [[32, 16]], 0, 0)
     iota("i3", [[1, 16], [0, 2]], 2288, -16)
     iota("i10", [[1, 16], [0, 16]], 1, 0)
@@ -271,43 +260,52 @@ def rank_program(g, core, T, topo):
     cp(("l1", 0, 32), ("t1", 0, 32))
     cp(("F", 15, 128, 16), ("B8", 0, 8))
     ts(("t2", 0, 16), ("i2", 0, 16), 511, A.bitwise_and)
+    fill(("C32", 0, 128), 1.0 / 8192)
+    fill(("PT", 0, 1), 0.0)
+    fill(("PT", 1, 2), 7.5)
+    fill(("PT", 2, 3), -0.5)
+    fill(("C1", 0, 128), -1.0 / 128)
+    fill(("CB", 0, 128), -BIG / 128)
+    fill(("y", 0, 16), BIG)
+    fill(("mm", 0, 16), BIG)
+    fill(("RS", 0, 256), 1.0)
+    fill(("RS", 0, 256, 16), 0.0)
+    ts(("FB", 0, 144), ("F", 0, 144), BIG, A.mult)
+    ts(("FhB", 0, 144), ("F", 0, 144), 0.5 * BIG, A.mult)
     cp(("wf", 0, 1), ("wti", 0, 1))
     tt(("t2", 16, 32), ("t2", 0, 16), ("p16", 0, 16), A.add)
-    ts(("Fw", 0, 144), ("F", 0, 144), ("wf", 0, 1), A.mult)
+    ts(("Fw", 0, 144), ("F", 0, 144), ("wf", 0, 1), A.mult, 1.0 / 2048, A.mult)
     cp(("l2", 0, 16), ("t2", 16, 32))
 
-    ts(("X", 0, 512), (("EL", 0, 256), ("l1", 0, 32)), 1184.0, A.add)
-    fold(("pu", 0, 16), "Fw", Z[0], 256, 512)
-    cp(("vi", 0, 16), ("pu", 0, 16))
+    ts(("X", 0, 512), (("EL", 0, 256), ("l1", 0, 32)), 1184.0, A.add, 2048.0, A.mult)
+    usum("pu", 0, 16, Z[0], 256, 512)
+    ts(("vi", 0, 16), ("pu", 0, 16), FLOOR, A.add)
     op("v", lambda e: e.transpose(T.XT[:, :], T.X[:, :]), [("X", 0, 512)], [("XT", 0, 512)])
-    ts(("va", 0, 16), ("vi", 0, 16), 2047, A.bitwise_and)
+    tt(("v", 0, 16), ("pu", 0, 16), ("vi", 0, 16), A.subtract)
     cp((E[0], 0, 256), (("XT", 0, 512), ("l2", 0, 16)))
-    ts(("v", 0, 16), ("va", 0, 16), 32.0, A.add)
     tt(("P", 0, 256), (("v", 0, 16), ("cl", 0, 16)), (E[0], 0, 256), A.mult)
     h = hlist("P", "N", "off", 0, 256)
     h[0]()
     ts(("Fh", 0, 144), ("F", 0, 144), 0.5, A.mult)
     h[1]()
 
-    fill(("PT", 0, 1), 0.0)
-    fill(("PT", 1, 2), 7.5)
     tt(("jb", 0, 16), ("pm", 0, 16), ("i8", 0, 16), A.add)
     ts(("NI", 0, 128), ("ID", 0, 128), -1.0, A.mult)
     cp(("pmf", 0, 1), ("pm", 0, 1))
-    fill(("C8", 0, 128), -1.0 / 16)
-    fill(("C1", 0, 128), -1.0 / 128)
     ts(("t1", 0, 16), ("i5", 0, 16), 255, A.bitwise_and)
     ts(("t1", 16, 32), ("i6", 0, 16), 255, A.bitwise_and)
     ts(("KC", 0, 256), ("i9", 0, 256), ("pmf", 0, 1), A.add, 2048.0, A.mult)
     cp(("pn", 0, 16), ("t1", 0, 16))
     cp(("p2", 0, 16), ("t1", 16, 32))
-    ts(("KC", 0, 256), ("KC", 0, 256), -1184.0, A.add)
-    fill(("y", 0, 16), BIG)
-    fill(("RS", 0, 256), 1.0)
-    fill(("RS", 0, 256, 16), 0.0)
+    ts(("KC", 0, 256), ("KC", 0, 256), 0.5, A.add)
+    cp(("IF", 0, 128), ("ID", 0, 128))
+    cp(("JF", 0, 128), ("NI", 0, 128))
+
+    def codes():
+        tt(("Rk", 0, 256), (("N", 0, 256), ("pn", 0, 16)), ("KC", 0, 256), A.add)
 
     def consts2():
-        ts(("TH", 0, 256), ("i10", 0, 256), 524288.0, A.mult, 864.0, A.add)
+        ts(("TH", 0, 256), ("i10", 0, 256), 524288.0, A.mult)
         ts(("ci", 0, 16), ("jb", 0, 16), 148.0, A.add)
         ts(("p31", 0, 16), ("ip", 0, 16), 31, A.bitwise_and)
         ts(("t1", 0, 16), ("ci", 0, 16), 255, A.bitwise_and)
@@ -322,7 +320,24 @@ def rank_program(g, core, T, topo):
         act(("Z4", 256, 512), src, AF.Copy)
         act(("Z4", 512, 1024), ("Z4", 0, 512), AF.Copy)
 
+    def tcol():
+        act(("Tt", 0, 240), ("ON", 0, 240), AF.Copy, None, ("PT", 1, 2))
+        act(("Th", 0, 240), ("ON", 0, 240), AF.Copy, None, ("PT", 2, 3))
+
+    def shift(e, lo, hi):
+        a, b = 16 * lo, 16 * hi
+
+        def fn(x):
+            x.matmul(T.d2[:, a - 16:b - 16], T.IF[:, :], T[e][:, a:b], True, False)
+            x.matmul(T.d2[:, a - 16:b - 16], T.JF[:, :], T[e][:, a - 16:b - 16], False, True)
+            return x.matmul(T.d2[:, 240 + a:240 + b], T.IF[:, :], T[e][:, a - 16:b - 16], True, True)
+        op("p", fn, [("IF", 0, 128), ("JF", 0, 128), (e, a - 16, b)], [("d2", a - 16, b - 16), ("d2", 240 + a, 240 + b)])
+
+    codes()
+    shift(E[0], 1, 16)
     z4((Z[0], 256, 512))
+    tcol()
+    late = []
 
     for t in range(RO):
         ec, en, zc, zn = E[t % 2], E[(t + 1) % 2], Z[t % 2], Z[(t + 1) % 2]
@@ -333,48 +348,13 @@ def rank_program(g, core, T, topo):
 
         def absq(lo, hi):
             act(("ZK", 256 * lo + 256, 256 * hi + 256), ("DF", 256 * lo, 256 * hi), AF.Abs)
-            fold(("pU", 16 * lo, 16 * hi), "Fw", "ZK", 256 * lo + 256, 256 * hi + 256)
+            usum("pU", 16 * lo, 16 * hi, "ZK", 256 * lo + 256, 256 * hi + 256)
 
         def sgn(lo, hi):
             act(("SG", 256 * lo, 256 * hi), ("DF", 256 * lo, 256 * hi), AF.Sign, -0.5)
 
         def cnta(lo, hi):
-            fold(("pa", 16 * lo, 16 * hi), "Fh", "SG", 256 * lo, 256 * hi)
-
-        g1(15)
-        sgn(15, 16)
-        act((zc, 0, 256), ("DF", 3840, 4096), AF.Abs)
-        fold(("pu", 32, 48), "Fh", "SG", 3840, 4096)
-        act(("Tt", 0, 240), ("ON", 0, 240), AF.Copy, None, ("PT", 1, 2))
-        g1(11, 15)
-        absq(11, 15)
-        ts(("a0c", 0, 16), ("pu", 32, 48), ("PT", 0, 1), A.is_lt, 256.0, A.mult)
-        sgn(11, 15)
-        cnta(11, 15)
-        g1(10)
-        tt(("o0i", 0, 16), ("a0c", 0, 16), ("jb", 0, 16), A.add)
-        g1(9)
-        cp(("o0u", 0, 16), ("o0i", 0, 16))
-        ts(("SIG", 0, 16), ("a0c", 0, 16), 1.0 / 128, A.mult, -1.0, A.add)
-        g1(8)
-        cp(("ZK", 0, 256), ((zc, 0, 512), ("o0u", 0, 16)))
-        fold(("pu", 64, 80), "Fw", "ZK", 0, 256)
-        absq(8, 11)
-        g1(4, 8)
-        absq(4, 8)
-        cp(("wi", 0, 16), ("pu", 64, 80))
-        g1(3)
-        ts(("wa", 0, 16), ("wi", 0, 16), 2047, A.bitwise_and)
-        g1(2)
-        ts(("w", 0, 16), ("wa", 0, 16), 32.0, A.add)
-        g1(1)
-        tt(("Pc", 0, 240), (("w", 0, 16), ("cl", 0, 15)), (ec, 0, 240), A.mult)
-        h = hlist("Pc", "Nc", "offc", 0, 240)
-        g1(0)
-        absq(0, 4)
-        h[0]()
-        tt(("Rk", 0, 256), (("N", 0, 256), ("pn", 0, 16)), ("KC", 0, 256), A.add)
-        h[1]()
+            fold(("pa", 16 * lo, 16 * hi), "FhB", "SG", 256 * lo, 256 * hi, (("CB", 0, 128), ("Th", 0, 16 * (hi - lo))))
 
         def cv(q):
             tt(("CC", 256 * q, 256 * q + 256), (DALL, ("offc", 16 * q, 16 * q + 16)), ("ZK", 0, 256), A.is_gt)
@@ -384,7 +364,7 @@ def rank_program(g, core, T, topo):
         def sgath(n):
             lo, hi = pairs[n]
             act(("DG", 256 * lo, 256 * hi), (DALL, ("offc", 16 * lo, 16 * hi)), AF.Copy)
-            bank = "d%d" % (n % 3)
+            bank = "d%d" % (n % 2)
 
             def fn(e):
                 for k in range(hi - lo):
@@ -396,60 +376,94 @@ def rank_program(g, core, T, topo):
 
         def ssign(n):
             lo, hi = pairs[n]
-            act(("CC", 256 * lo, 256 * hi), ("d%d" % (n % 3), 0, 256 * (hi - lo)), AF.Sign, -0.5)
-
-        vq = list(range(14, NS - 1, -1))
-        chain = [lambda: cp(("Ui", 0, 240), ("pU", 0, 240)),
-                 lambda: ts(("Ua", 0, 240), ("Ui", 0, 240), 2047, A.bitwise_and),
-                 lambda: ts(("Ub", 0, 240), ("Ua", 0, 240), 32.0, A.add),
-                 lambda: tt(("Pb", 0, 240), ((ec, 240, 256), ("cl", 0, 15)), ("Ub", 0, 240), A.mult)]
-        half = len(pairs) // 2
-        for n in range(half):
-            sgath(n)
-            if n:
-                ssign(n - 1)
-        for n, q in enumerate(vq):
-            cv(q)
-            if len(vq) - n <= len(chain):
-                chain[len(chain) - (len(vq) - n)]()
-        fold(("pc", 16 * NS, 240), "F", "CC", 256 * NS, 3840, (("C8", 0, 128), ("ON", 0, 240 - 16 * NS)))
-        for n in range(half, len(pairs)):
-            sgath(n)
-            ssign(n - 1)
-        sgn(8, 11)
-        ssign(len(pairs) - 1)
-        cnta(8, 11)
-        fold(("pc", 0, 16 * NS), "Fh", "CC", 0, 256 * NS)
-        h = hlist("Pb", "Nb", "offb", 0, 240)
-        h[0]()
-        h[1]()
+            act(("CC", 256 * lo, 256 * hi), ("d%d" % (n % 2), 0, 256 * (hi - lo)), AF.Sign, -0.5)
 
         def bv(lo, hi):
             tt(("BB", 256 * lo, 256 * hi), (DALL, ("offb", 16 * lo, 16 * hi)), ("ZK", 256 * lo + 256, 256 * hi + 256), A.is_gt)
             fold(("pb", 16 * lo, 16 * hi), "F", "BB", 256 * lo, 256 * hi, (("C1", 0, 128), ("Tt", 0, 16 * (hi - lo))))
 
+        g1(15)
+        for f in late:
+            f()
+        sgn(15, 16)
+        act((zc, 0, 256), ("DF", 3840, 4096), AF.Abs)
+        fold(("pu", 32, 48), "Fh", "SG", 3840, 4096)
+        g1(12, 15)
+        absq(12, 15)
+        ts(("a0c", 0, 16), ("pu", 32, 48), ("PT", 0, 1), A.is_lt, 256.0, A.mult)
+        sgn(12, 15)
+        g1(11)
+        tt(("o0i", 0, 16), ("a0c", 0, 16), ("jb", 0, 16), A.add)
+        act(("SB", 0, 240), (("a0c", 0, 16), ("cl", 0, 15)), AF.Identity, -BIG, BIG / 128)
+        g1(10)
+        cp(("o0u", 0, 16), ("o0i", 0, 16))
+        g1(9)
+        cp(("ZK", 0, 256), ((zc, 0, 512), ("o0u", 0, 16)))
+        usum("pu", 64, 80, "ZK", 0, 256)
+        g1(7, 9)
+        absq(8, 12)
+        cnta(12, 15)
+        sgn(8, 12)
+        ts(("wi", 0, 16), ("pu", 64, 80), FLOOR, A.add)
+        g1(6)
+        tt(("w", 0, 16), ("pu", 64, 80), ("wi", 0, 16), A.subtract)
+        g1(4, 6)
+        absq(4, 8)
+        tt(("Pc", 0, 240), (("w", 0, 16), ("cl", 0, 15)), (ec, 0, 240), A.mult)
+        h = hlist("Pc", "Nc", "offc", 0, 240)
+        g1(3)
+        h[0]()
+        g1(2)
+        h[1]()
+        absq(2, 4)
+        g1(0, 2)
+        absq(0, 2)
+        sgath(0)
+        sgath(1)
+        ssign(0)
+        cnta(8, 12)
+        for n in range(2, len(pairs) - 1):
+            sgath(n)
+            ssign(n - 1)
+
+        chain = [lambda: ts(("Ui", 0, 240), ("pU", 0, 240), FLOOR, A.add),
+                 lambda: tt(("Ub", 0, 240), ("pU", 0, 240), ("Ui", 0, 240), A.subtract),
+                 lambda: tt(("Pb", 0, 240), ((ec, 240, 256), ("cl", 0, 15)), ("Ub", 0, 240), A.mult)]
+        vq = list(range(14, NS - 1, -1))
+        for n, q in enumerate(vq):
+            cv(q)
+            if len(vq) - n <= len(chain):
+                chain[len(chain) - (len(vq) - n)]()
+        fold(("pc", 16 * NS, 240), "FB", "CC", 256 * NS, 3840, (("CB", 0, 128), ("Tt", 0, 240 - 16 * NS)))
+        sgath(len(pairs) - 1)
+        ssign(len(pairs) - 2)
+        ssign(len(pairs) - 1)
+        h = hlist("Pb", "Nb", "offb", 0, 240)
+        h[0]()
+        h[1]()
+
         bv(0, 4)
-        sgn(0, 8)
-        cnta(0, 8)
-        act(("paS", 0, 240), ("pa", 0, 240), AF.Copy)
+        fold(("pc", 0, 16 * NS), "FhB", "CC", 0, 256 * NS, (("CB", 0, 128), ("Th", 0, 16 * NS)))
         bv(4, 8)
+        sgn(4, 8)
+        cnta(4, 8)
+        sgn(0, 4)
+        cnta(0, 4)
+        act(("pcS", 0, 240), ("pc", 0, 240), AF.Copy)
         bv(8, 12)
         bv(12, 15)
-        tt(("dE", 0, 240), (ec, 16, 256), (ec, 0, 240), A.subtract)
-        tt(("mm", 0, 240), ("pc", 0, 240), ("paS", 0, 240), A.min)
-        ts(("Q1", 0, 240), ("mm", 0, 240), ("PT", 0, 1), A.is_ge, BIG, A.mult)
-        tt(("Q", 0, 240), (("SIG", 0, 16), ("cl", 0, 15)), ("Q1", 0, 240), A.mult)
+        tt(("mm", 16, 256), ("pa", 0, 240), ("pcS", 0, 240), A.min)
+        tt(("Rg", 0, 256), (("mm", 0, 256), ("p2", 0, 16)), ("Rk", 0, 256), A.min)
 
-        tt(("y", 16, 256), ("pb", 0, 240), ("Q", 0, 240), A.mult)
-        tt(("x", 0, 256), (("y", 0, 256), ("p2", 0, 16)), ("Rk", 0, 256), A.min)
+        tt(("y", 16, 256), ("pb", 0, 240), ("SB", 0, 240), A.mult)
+        tt(("x", 0, 256), (("y", 0, 256), ("p2", 0, 16)), ("Rg", 0, 256), A.min)
         op("v", lambda e: e.tensor_tensor_scan(T.Sc[:, :], T.RS[:, :], T.x[:, :], 0.0, A.mult, A.max),
            [("RS", 0, 256), ("x", 0, 256)], [("Sc", 0, 256)])
         sv = ("Sc", 15, 256, 16)
-        ts(("Oi", 0, 16), sv, -864.0, A.add)
-        cp(("Ni", 0, 16), sv)
-        ts(("Oj", 0, 16), ("Oi", 0, 16), 11, A.logical_shift_right)
-        ts(("LH", 0, 16), ("Ni", 0, 16), 7, A.bitwise_and)
+        ts(("Oj", 0, 16), sv, -1024.0, A.add, 1.0 / 2048, A.mult)
+        ts(("Ni", 0, 16), sv, 863.5, A.add)
         cp(("ou", 0, 16), ("Oj", 0, 16))
+        ts(("LH", 0, 16), ("Ni", 0, 16), 7, A.bitwise_and)
         ts(("LH", 16, 32), ("Ni", 0, 16), 3, A.logical_shift_right, 255, A.bitwise_and)
         cp((zn, 256, 512), (("ZK", 0, 4096), ("ou", 0, 16)))
         cp((zn, 512, 544), ("LH", 0, 32))
@@ -473,26 +487,26 @@ def rank_program(g, core, T, topo):
         if last:
             dma("y", "yz", T.yz[:, :], T[zn][:, 256:512], [(zn, 256, 512)], [])
         else:
-            fold(("pu", 0, 16), "Fw", zn, 256, 512)
+            usum("pu", 0, 16, zn, 256, 512)
             z4((zn, 256, 512))
         if t == 0:
             consts2()
-        ts(("NB", 0, 16), sv, 525152.0, A.is_lt, 67108864.0, A.mult)
+        ts(("NB", 0, 16), sv, 524288.0, A.is_lt, 67108864.0, A.mult)
         if not last:
-            ts(("fl", 0, 16), sv, 525152.0, A.is_ge)
+            ts(("fl", 0, 16), sv, 524288.0, A.is_ge)
             op("p", lambda e: e.matmul(T.pu[:, 96:112], T.ON[:, 0:128], T.fl[:, :], True, True),
                [("ON", 0, 128), ("fl", 0, 16)], [("pu", 96, 112)])
         tt(("S3", 0, 16), sv, ("NB", 0, 16), A.add)
         tt(("keep", 0, 240), (("S3", 0, 16), ("cl", 0, 15)), ("TH", 16, 256), A.is_lt)
         if not last:
-            cp(("vi", 0, 16), ("pu", 0, 16))
-        tt(("kd", 0, 240), ("keep", 0, 240), ("dE", 0, 240), A.mult)
+            ts(("vi", 0, 16), ("pu", 0, 16), FLOOR, A.add)
+        tt(("kd", 0, 240), ("keep", 0, 240), ("d2", 0, 240), A.mult)
         if not last:
-            ts(("va", 0, 16), ("vi", 0, 16), 2047, A.bitwise_and)
-        tt((en, 16, 256), ("kd", 0, 240), (ec, 0, 240), A.add)
+            tt(("v", 0, 16), ("pu", 0, 16), ("vi", 0, 16), A.subtract)
+        tt((en, 16, 256), ("kd", 0, 240), ("d2", 256, 496), A.add)
         if not last:
-            ts(("v", 0, 16), ("va", 0, 16), 32.0, A.add)
-            op("v", lambda e: e.tensor_reduce(T.As[:, :], T.pu[:, 96:112], AxisListType.X, A.add), [("pu", 96, 112)], [("As", 0, 1)])
+            op("s", lambda e: e.activation(T.jk[:, :], T.pu[:, 96:112], AF.Identity, accum_out=T.As[:, :]), [("pu", 96, 112)],
+               [("jk", 0, 16), ("As", 0, 1)])
             tt(("P", 16, 256), (("v", 0, 16), ("cl", 0, 15)), (en, 16, 256), A.mult)
             cp(("Ai", 0, 1), ("As", 0, 1))
             h = hlist("P", "N", "off", 16, 256)
@@ -500,24 +514,29 @@ def rank_program(g, core, T, topo):
             ts(("Aj", 0, 1), ("Ai", 0, 1), 1, A.bitwise_and)
             h[1]()
             cp(("PT", 0, 1), ("Aj", 0, 1))
-            ts(("PT", 1, 2), ("Aj", 0, 1), 7.5, A.add)
+            act(("PT", 1, 2), ("PT", 0, 1), AF.Identity, 7.5)
+            act(("PT", 2, 3), ("PT", 0, 1), AF.Identity, -0.5)
+            tcol()
+            shift(en, 2, 16)
+            codes()
         else:
             cp(("X", 0, 512), ((en, 0, 256), ("l3", 0, 32)))
 
         tt(("ci", 0, 16), (lc, 256, 272), ("cb", 0, 16), A.add)
         ts(("e15", 0, 16), (lc, 272, 288), 8.0, A.mult, 1184.0, A.add)
         cp(("cu", 0, 16), ("ci", 0, 16))
-        tt((en, 0, 16), ("e15", 0, 16), (lc, 256, 272), A.add)
+        tt(("e16", 0, 16), ("e15", 0, 16), (lc, 256, 272), A.add)
         tt(("su", 0, 256), (DALL, ("cu", 0, 16)), (lc, 0, 256), A.add)
+        ts((en, 0, 16), ("e16", 0, 16), 2048.0, A.mult)
+        ts(("sh", 0, 256), ("su", 0, 256), 1, A.logical_shift_right)
         if not last:
             tt(("P", 0, 16), ("v", 0, 16), (en, 0, 16), A.mult)
-        ts(("sh", 0, 256), ("su", 0, 256), 1, A.logical_shift_right)
+        cp((DALL, ("cu", 0, 16)), ("sh", 0, 256))
         if not last:
             h = hlist("P", "N", "off", 0, 16)
             h[0]()
-        cp((DALL, ("cu", 0, 16)), ("sh", 0, 256))
-        if not last:
-            h[1]()
+            shift(en, 1, 2)
+            late = [h[1], lambda: tt(("Rk", 1, 256, 16), ("N", 0, 16), ("KC", 1, 256, 16), A.add)]
             continue
 
         dma("y", "yda", T.yd[:, 864:2048], T.D[:, 0:1184], [("D", 0, 1184)], [])
@@ -525,7 +544,7 @@ def rank_program(g, core, T, topo):
         cp(("X", 15, 512, 32), (en, 0, 16))
         cp(("X", 31, 512, 32), (en, 0, 16))
         op("v", lambda e: e.transpose(T.XT[:, :], T.X[:, :]), [("X", 0, 512)], [("XT", 0, 512)])
-        ts(("YL", 0, 256), (("XT", 0, 512), ("l4", 0, 16)), -1184.0, A.add)
+        ts(("YL", 0, 256), (("XT", 0, 512), ("l4", 0, 16)), 1.0 / 2048, A.mult, -1184.0, A.add)
         dma("y", "ye", T.ye[:, :], T.YL[:, :], [("YL", 0, 256)], [])
 
     for s in sorted(total):

import numpy as np
from concourse.mybir import AluOpType as A
from concourse.mybir import ActivationFunctionType as AF

RO = 5
NS = 8
NENG = 8
PAY = 288
BIG = 2.0 ** 25
FLOOR = -1055.5 / 2048


def _s(n, dt):
    return ("sbuf", [128, n], dt)


SCRATCH = {
    "Ea": _s(256, "float32"), "Eb": _s(256, "float32"),
    "Za": _s(544, "bfloat16"), "Zb": _s(544, "bfloat16"),
}
for _n, _w in (("D", 2048), ("Z4", 1024),
               ("ZK", 4096),
               ("DF", 4096), ("SG", 4096),
               ("CC", 3840), ("BB", 3840),
               ("DG", 256 * NS),
               ("Tt", 240), ("Th", 240),
               ("fl", 16), ("O8", 8), ("B8a", 8), ("B8", 8), ("F", 144), ("Fh", 144), ("Fw", 144), ("FB", 144), ("FhB", 144),
               ("ON", 256), ("ID", 128), ("NI", 128), ("C1", 128), ("CB", 128), ("C32", 128)):
    SCRATCH[_n] = _s(_w, "bfloat16")
for _n, _w in (("v", 16), ("w", 16), ("Ub", 240), ("a0c", 16), ("SB", 240), ("Rk", 256), ("Rg", 256), ("pcS", 240), ("mm", 256),
               ("y", 256), ("x", 256), ("Sc", 256), ("NB", 16), ("S3", 16), ("keep", 240), ("kd", 240), ("As", 1), ("jk", 16),
               ("PT", 3),
               ("e15", 16), ("e16", 16), ("X", 512), ("XT", 512), ("YL", 256), ("wf", 1), ("IF", 128), ("JF", 128), ("pmf", 1),
               ("jb", 16), ("cb", 16), ("KC", 256), ("TH", 256), ("RS", 256)):
    SCRATCH[_n] = _s(_w, "float32")
for _n, _w in (("N", 256), ("P", 256), ("Nc", 240), ("Pc", 240), ("Nb", 240), ("Pb", 240), ("Ui", 240), ("vi", 16), ("wi", 16),
               ("o0i", 16), ("Oj", 16), ("Ni", 16), ("LH", 32), ("Ai", 1), ("Aj", 1), ("ci", 16), ("su", 256), ("sh", 256),
               ("EL", 256), ("wti", 1), ("ip", 32), ("pm", 32), ("p16", 16), ("p31", 16), ("i1", 32), ("i2", 16), ("i3", 32),
               ("i4", 16), ("i5", 16), ("i6", 16), ("i8", 16), ("i9", 256), ("i10", 256), ("t1", 32), ("t2", 32)):
    SCRATCH[_n] = _s(_w, "int32")
for _n, _w in (("off", 256), ("offc", 240), ("offb", 240), ("o0u", 16), ("ou", 16), ("cu", 16), ("cl", 16), ("l1", 32),
               ("l2", 16), ("l3", 32), ("l4", 16), ("pn", 16), ("p2", 16)):
    SCRATCH[_n] = _s(_w, "uint16")
PSUM = ["pu", "pa", "pU", "pc", "pb", "d0", "d1", "d2"]
for _n in PSUM:
    SCRATCH[_n] = ("psum", [128, 512], "float32")
for _t in range(RO):
    SCRATCH["L%d" % _t] = _s(PAY, "bfloat16")
    SCRATCH["R%d" % _t] = _s(PAY, "bfloat16")
DMAS = ["wt", "zv", "ef", "da", "db", "yda", "ydb", "ye", "yz"]
SEMAPHORES = (["qv", "qs", "qp", "qg"] + ["dma_" + k for k in DMAS] +
              ["arr%d" % t for t in range(RO)] + ["rl%d" % t for t in range(RO)] + ["loc%d" % t for t in range(RO)])


def target(cores, rank, t):
    return cores[(rank + 1 + t % 3) % len(cores)]


def route(topo, src, dst):
    if topo.may_write(src, dst):
        return src
    cand = [c for c in topo.cores_of(src) if c != src and topo.may_write(c, dst)]
    same = [c for c in cand if topo.die(c) == topo.die(src)]
    return (same or cand)[0]


def engines(topo, src, dst):
    e = topo.engines(src, dst)[:NENG]
    return sum(1 << k for k in e), len(e)


def relay_program(g, core, T, topo):
    used = []
    for t in range(RO):
        for r in range(len(T.cores)):
            src, dst = T.cores[r], target(T.cores, r, t)
            if src != core and route(topo, src, dst) == core:
                m, n = engines(topo, core, dst)
                _, nin = engines(topo, src, core)
                rid, pid = topo.addr(dst, core)
                g.wait_ge(T.sem["rl%d" % t], nin)
                g.remote_dma(T["L%d" % t][:, :], T["R%d" % t][:, :], T.sem["arr%d" % t], T.sem["loc%d" % t], pid, rid, m)
                used.append((t, n))
    for t, n in used:
        g.wait_ge(T.sem["loc%d" % t], n)


def rank_program(g, core, T, topo):
    rank = T.rank_of(core)
    if rank is None:
        relay_program(g, core, T, topo)
        return
    cores = T.cores
    eng = {"v": g.vector, "s": g.scalar, "p": g.tensor, "g": g, "y": g.sync}
    known = {k: {} for k in eng}
    snap, acc, total = {}, {}, {}

    def wait(q, tok):
        s, n = tok
        if known[q].get(s, 0) >= n:
            return
        eng[q].wait_ge(T.sem[s], n)
        for a, b in snap.get(tok, {}).items():
            if known[q].get(a, 0) < b:
                known[q][a] = b
        known[q][s] = n

    def before(q, reads, writes):
        need = {}
        for regs, wr in ((reads, False), (writes, True)):
            for b, lo, hi in regs:
                ps = b in PSUM
                for l2, h2, w2, tok, q2 in acc.get(b, []):
                    if ps:
                        hit = (q2 != q) or (q != "p" and (wr or w2) and lo < h2 and l2 < hi)
                    else:
                        hit = (wr or w2) and lo < h2 and l2 < hi
                    if hit and need.get(tok[0], 0) < tok[1]:
                        need[tok[0]] = tok[1]
        for s in sorted(need):
            wait(q, (s, need[s]))

    def after(q, reads, writes, tok):
        snap[tok] = dict(known[q])
        for b, lo, hi in writes:
            l = acc.get(b, [])
            acc[b] = [r for r in l if not (lo <= r[0] and r[1] <= hi and b not in PSUM)] + [(lo, hi, True, tok, q)]
        for b, lo, hi in reads:
            l = acc.setdefault(b, [])
            acc[b] = [r for r in l if not (r[4] == q and not r[2] and lo <= r[0] and r[1] <= hi and r[3][0] == tok[0])] + [(lo, hi, False, tok, q)]
        for b, lo, hi in list(reads) + list(writes):
            if b in PSUM:
                last = {}
                for r in acc[b]:
                    last[(r[4], r[2], r[0], r[1])] = r
                acc[b] = list(last.values())

    def op(q, fn, reads, writes):
        before(q, reads, writes)
        s = "q" + q
        total[s] = total.get(s, 0) + 1
        fn(eng[q]).then_inc(T.sem[s], 1)
        after(q, reads, writes, (s, total[s]))

    def dma(q, name, out, in_, reads, writes):
        before(q, reads, writes)
        s = "dma_" + name
        eng[q].dma_start(out, in_).then_inc(T.sem[s], 16)
        total[s] = 16
        after(q, reads, writes, (s, 16))

    def ap(v):
        return T[v[0]][:, v[1]:v[2]] if len(v) == 3 else T[v[0]][:, v[1]:v[2]:v[3]]

    def rg(v):
        return (v[0], v[1], v[2])

    def opnd(v):
        if isinstance(v[0], tuple):
            return ap(v[0]).indirect(ap(v[1])), [rg(v[0]), rg(v[1])]
        return ap(v), [rg(v)]

    def tt(out, a, b, o):
        oa, orr = opnd(out)
        aa, ar = opnd(a)
        ba, br = opnd(b)
        op("v", lambda e: e.tensor_tensor(oa, aa, ba, o), ar + br + orr[1:], orr[:1])

    def ts(out, a, s1, o1, s2=None, o2=None):
        oa, orr = opnd(out)
        aa, ar = opnd(a)
        rd = list(ar)
        sc = []
        for s in (s1, s2):
            if isinstance(s, tuple):
                rd.append(rg(s))
                sc.append(ap(s))
            else:
                sc.append(s)
        if o2 is None:
            op("v", lambda e: e.tensor_scalar(oa, aa, sc[0], None, o1), rd, orr[:1])
        else:
            op("v", lambda e: e.tensor_scalar(oa, aa, sc[0], sc[1], o1, o2), rd, orr[:1])

    def cp(out, a):
        oa, orr = opnd(out)
        aa, ar = opnd(a)
        op("v", lambda e: e.tensor_copy(oa, aa), ar + orr[1:], orr[:1])

    def fill(out, c):
        op("v", lambda e: e.memset(ap(out), c), [], [rg(out)])

    def act(out, a, f, bias=None, scale=None):
        aa, ar = opnd(a)
        kw = {}
        rd = list(ar)
        for k, c in (("bias", bias), ("scale", scale)):
            if isinstance(c, tuple):
                kw[k] = ap(c)
                rd.append(rg(c))
            elif c is not None:
                kw[k] = c
        op("s", lambda e: e.activation(ap(out), aa, f, **kw), rd, [rg(out)])

    def fold(out, fm, src, lo, hi, *extra):
        reads = [(fm, 0, 144), (src, lo, hi)]
        for x in extra:
            reads += [rg(x[0]), rg(x[1])]

        def fn(e):
            for x in extra:
                e.matmul(ap(out), ap(x[0]), ap(x[1]), x is extra[0], False)
            for jl in range(16):
                r = e.matmul(ap(out), T[fm][:, 15 - jl:143 - jl], T[src][:, lo + jl:hi:16], jl == 0 and not extra, jl == 15)
            return r
        op("p", fn, reads, [rg(out)])

    def usum(bank, lo, hi, src, slo, shi):
        fold((bank, lo, hi), "Fw", src, slo, shi, (("C32", 0, 128), ("ON", 0, hi - lo)))

    def hlist(P, N, off, lo, hi):
        return [lambda: ts((N, lo, hi), (P, lo, hi), 5, A.logical_shift_right, 2047, A.bitwise_and),
                lambda: cp((off, lo, hi), (N, lo, hi))]

    E = ["Ea", "Eb"]
    Z = ["Za", "Zb"]
    DALL = ("D", 0, 2048)

    dma("s", "ef", T.EL[:, :], T.ef[:, :], [], [("EL", 0, 256)])
    dma("y", "wt", T.wti[:, :], T.wt[:, :], [], [("wti", 0, 1)])
    dma("y", "zv", T[Z[0]][:, 256:512], T.zv[:, :], [], [(Z[0], 256, 512)])
    dma("s", "da", T.D[:, 1184:2048], T.dv[:, 0:864], [], [("D", 1184, 2048)])
    dma("y", "db", T.D[:, 0:1184], T.dv[:, 864:2048], [], [("D", 0, 1184)])

    def iota(name, pattern, base, cm):
        n = SCRATCH[name][1][1]
        op("g", lambda e: e.iota(T[name][:, :], pattern, base, cm), [], [(name, 0, n)])

    fill(("O8", 0, 8), 1.0)
    fill(("F", 0, 144), 0.0)
    fill(("ON", 0, 256), 1.0)
    iota("ip", [[0, 32]], 0, 1)
    iota("i1", [[16, 16], [0, 2]], 0, 0)
    op("g", lambda e: e.affine_select(T.B8a[:, :], T.O8[:, :], [[-16, 8]], A.is_ge, 0.0, 0, 1), [("O8", 0, 8)], [("B8a", 0, 8)])
    op("g", lambda e: e.affine_select(T.B8[:, :], T.B8a[:, :], [[16, 8]], A.is_ge, 0.0, 15, -1), [("B8a", 0, 8)], [("B8", 0, 8)])
    iota("i2", [[-1, 16]], 15, 32)
    iota("i5", [[1, 16]], 240, 16)
    iota("i6", [[1, 16]], 0, 16)
    iota("i8", [[16, 16]], 0, 0)
    op("g", lambda e: e.affine_select(T.ID[:, :], T.ON[:, 0:128], [[-1, 128]], A.is_equal, 0.0, 0, 1), [("ON", 0, 128)], [("ID", 0, 128)])
    iota("i9", [[16, 16], [256, 16]], 0, 0)
    iota("i4", [[32, 16]], 0, 0)
    iota("i3", [[1, 16], [0, 2]], 2288, -16)
    iota("i10", [[1, 16], [0, 16]], 1, 0)

    ts(("pm", 0, 32), ("ip", 0, 32), 15, A.bitwise_and)
    ts(("p16", 0, 16), ("ip", 0, 16), 16, A.bitwise_and)
    tt(("t1", 0, 32), ("pm", 0, 32), ("i1", 0, 32), A.add)
    cp(("cl", 0, 16), ("pm", 0, 16))
    cp(("l1", 0, 32), ("t1", 0, 32))
    cp(("F", 15, 128, 16), ("B8", 0, 8))
    ts(("t2", 0, 16), ("i2", 0, 16), 511, A.bitwise_and)
    fill(("C32", 0, 128), 1.0 / 8192)
    fill(("PT", 0, 1), 0.0)
    fill(("PT", 1, 2), 7.5)
    fill(("PT", 2, 3), -0.5)
    fill(("C1", 0, 128), -1.0 / 128)
    fill(("CB", 0, 128), -BIG / 128)
    fill(("y", 0, 16), BIG)
    fill(("mm", 0, 16), BIG)
    fill(("RS", 0, 256), 1.0)
    fill(("RS", 0, 256, 16), 0.0)
    ts(("FB", 0, 144), ("F", 0, 144), BIG, A.mult)
    ts(("FhB", 0, 144), ("F", 0, 144), 0.5 * BIG, A.mult)
    cp(("wf", 0, 1), ("wti", 0, 1))
    tt(("t2", 16, 32), ("t2", 0, 16), ("p16", 0, 16), A.add)
    ts(("Fw", 0, 144), ("F", 0, 144), ("wf", 0, 1), A.mult, 1.0 / 2048, A.mult)
    cp(("l2", 0, 16), ("t2", 16, 32))

    ts(("X", 0, 512), (("EL", 0, 256), ("l1", 0, 32)), 1184.0, A.add, 2048.0, A.mult)
    usum("pu", 0, 16, Z[0], 256, 512)
    ts(("vi", 0, 16), ("pu", 0, 16), FLOOR, A.add)
    op("v", lambda e: e.transpose(T.XT[:, :], T.X[:, :]), [("X", 0, 512)], [("XT", 0, 512)])
    tt(("v", 0, 16), ("pu", 0, 16), ("vi", 0, 16), A.subtract)
    cp((E[0], 0, 256), (("XT", 0, 512), ("l2", 0, 16)))
    tt(("P", 0, 256), (("v", 0, 16), ("cl", 0, 16)), (E[0], 0, 256), A.mult)
    h = hlist("P", "N", "off", 0, 256)
    h[0]()
    ts(("Fh", 0, 144), ("F", 0, 144), 0.5, A.mult)
    h[1]()

    tt(("jb", 0, 16), ("pm", 0, 16), ("i8", 0, 16), A.add)
    ts(("NI", 0, 128), ("ID", 0, 128), -1.0, A.mult)
    cp(("pmf", 0, 1), ("pm", 0, 1))
    ts(("t1", 0, 16), ("i5", 0, 16), 255, A.bitwise_and)
    ts(("t1", 16, 32), ("i6", 0, 16), 255, A.bitwise_and)
    ts(("KC", 0, 256), ("i9", 0, 256), ("pmf", 0, 1), A.add, 2048.0, A.mult)
    cp(("pn", 0, 16), ("t1", 0, 16))
    cp(("p2", 0, 16), ("t1", 16, 32))
    ts(("KC", 0, 256), ("KC", 0, 256), 0.5, A.add)
    cp(("IF", 0, 128), ("ID", 0, 128))
    cp(("JF", 0, 128), ("NI", 0, 128))

    def codes():
        tt(("Rk", 0, 256), (("N", 0, 256), ("pn", 0, 16)), ("KC", 0, 256), A.add)

    def consts2():
        ts(("TH", 0, 256), ("i10", 0, 256), 524288.0, A.mult)
        ts(("ci", 0, 16), ("jb", 0, 16), 148.0, A.add)
        ts(("p31", 0, 16), ("ip", 0, 16), 31, A.bitwise_and)
        ts(("t1", 0, 16), ("ci", 0, 16), 255, A.bitwise_and)
        ts(("t2", 0, 32), ("i3", 0, 32), 255, A.bitwise_and)
        ts(("cb", 0, 16), ("t1", 0, 16), 8.0, A.mult)
        tt(("t1", 16, 32), ("p31", 0, 16), ("i4", 0, 16), A.add)
        cp(("l3", 0, 32), ("t2", 0, 32))
        cp(("l4", 0, 16), ("t1", 16, 32))

    def z4(src):
        act(("Z4", 0, 256), src, AF.Copy)
        act(("Z4", 256, 512), src, AF.Copy)
        act(("Z4", 512, 1024), ("Z4", 0, 512), AF.Copy)

    def tcol():
        act(("Tt", 0, 240), ("ON", 0, 240), AF.Copy, None, ("PT", 1, 2))
        act(("Th", 0, 240), ("ON", 0, 240), AF.Copy, None, ("PT", 2, 3))

    def shift(e, lo, hi):
        a, b = 16 * lo, 16 * hi

        def fn(x):
            x.matmul(T.d2[:, a - 16:b - 16], T.IF[:, :], T[e][:, a:b], True, False)
            x.matmul(T.d2[:, a - 16:b - 16], T.JF[:, :], T[e][:, a - 16:b - 16], False, True)
            return x.matmul(T.d2[:, 240 + a:240 + b], T.IF[:, :], T[e][:, a - 16:b - 16], True, True)
        op("p", fn, [("IF", 0, 128), ("JF", 0, 128), (e, a - 16, b)], [("d2", a - 16, b - 16), ("d2", 240 + a, 240 + b)])

    codes()
    shift(E[0], 1, 16)
    z4((Z[0], 256, 512))
    tcol()
    late = []

    for t in range(RO):
        ec, en, zc, zn = E[t % 2], E[(t + 1) % 2], Z[t % 2], Z[(t + 1) % 2]

        def g1(lo, hi=None):
            hi = hi or lo + 1
            tt(("DF", 256 * lo, 256 * hi), (DALL, ("off", 16 * lo, 16 * hi)), ("Z4", 0, 256 * (hi - lo)), A.subtract)

        def absq(lo, hi):
            act(("ZK", 256 * lo + 256, 256 * hi + 256), ("DF", 256 * lo, 256 * hi), AF.Abs)
            usum("pU", 16 * lo, 16 * hi, "ZK", 256 * lo + 256, 256 * hi + 256)

        def sgn(lo, hi):
            act(("SG", 256 * lo, 256 * hi), ("DF", 256 * lo, 256 * hi), AF.Sign, -0.5)

        def cnta(lo, hi):
            fold(("pa", 16 * lo, 16 * hi), "FhB", "SG", 256 * lo, 256 * hi, (("CB", 0, 128), ("Th", 0, 16 * (hi - lo))))

        def cv(q):
            tt(("CC", 256 * q, 256 * q + 256), (DALL, ("offc", 16 * q, 16 * q + 16)), ("ZK", 0, 256), A.is_gt)

        pairs = [(q, min(q + 2, NS)) for q in range(0, NS, 2)]

        def sgath(n):
            lo, hi = pairs[n]
            act(("DG", 256 * lo, 256 * hi), (DALL, ("offc", 16 * lo, 16 * hi)), AF.Copy)
            bank = "d%d" % (n % 2)

            def fn(e):
                for k in range(hi - lo):
                    o = ap((bank, 256 * k, 256 * k + 256))
                    e.matmul(o, T.NI[:, :], T.ZK[:, 0:256], True, False)
                    r = e.matmul(o, T.ID[:, :], T.DG[:, 256 * (lo + k):256 * (lo + k) + 256], False, True)
                return r
            op("p", fn, [("NI", 0, 128), ("ID", 0, 128), ("ZK", 0, 256), ("DG", 256 * lo, 256 * hi)], [(bank, 0, 256 * (hi - lo))])

        def ssign(n):
            lo, hi = pairs[n]
            act(("CC", 256 * lo, 256 * hi), ("d%d" % (n % 2), 0, 256 * (hi - lo)), AF.Sign, -0.5)

        def bv(lo, hi):
            tt(("BB", 256 * lo, 256 * hi), (DALL, ("offb", 16 * lo, 16 * hi)), ("ZK", 256 * lo + 256, 256 * hi + 256), A.is_gt)
            fold(("pb", 16 * lo, 16 * hi), "F", "BB", 256 * lo, 256 * hi, (("C1", 0, 128), ("Tt", 0, 16 * (hi - lo))))

        g1(15)
        for f in late:
            f()
        sgn(15, 16)
        act((zc, 0, 256), ("DF", 3840, 4096), AF.Abs)
        fold(("pu", 32, 48), "Fh", "SG", 3840, 4096)
        g1(12, 15)
        absq(12, 15)
        ts(("a0c", 0, 16), ("pu", 32, 48), ("PT", 0, 1), A.is_lt, 256.0, A.mult)
        sgn(12, 15)
        g1(11)
        tt(("o0i", 0, 16), ("a0c", 0, 16), ("jb", 0, 16), A.add)
        act(("SB", 0, 240), (("a0c", 0, 16), ("cl", 0, 15)), AF.Identity, -BIG, BIG / 128)
        g1(10)
        cp(("o0u", 0, 16), ("o0i", 0, 16))
        g1(9)
        cp(("ZK", 0, 256), ((zc, 0, 512), ("o0u", 0, 16)))
        usum("pu", 64, 80, "ZK", 0, 256)
        g1(7, 9)
        absq(8, 12)
        cnta(12, 15)
        sgn(8, 12)
        ts(("wi", 0, 16), ("pu", 64, 80), FLOOR, A.add)
        g1(6)
        tt(("w", 0, 16), ("pu", 64, 80), ("wi", 0, 16), A.subtract)
        g1(4, 6)
        absq(4, 8)
        tt(("Pc", 0, 240), (("w", 0, 16), ("cl", 0, 15)), (ec, 0, 240), A.mult)
        h = hlist("Pc", "Nc", "offc", 0, 240)
        g1(3)
        h[0]()
        g1(2)
        h[1]()
        absq(2, 4)
        g1(0, 2)
        absq(0, 2)
        sgath(0)
        sgath(1)
        ssign(0)
        cnta(8, 12)
        for n in range(2, len(pairs) - 1):
            sgath(n)
            ssign(n - 1)

        chain = [lambda: ts(("Ui", 0, 240), ("pU", 0, 240), FLOOR, A.add),
                 lambda: tt(("Ub", 0, 240), ("pU", 0, 240), ("Ui", 0, 240), A.subtract),
                 lambda: tt(("Pb", 0, 240), ((ec, 240, 256), ("cl", 0, 15)), ("Ub", 0, 240), A.mult)]
        vq = list(range(14, NS - 1, -1))
        for n, q in enumerate(vq):
            cv(q)
            if len(vq) - n <= len(chain):
                chain[len(chain) - (len(vq) - n)]()
        fold(("pc", 16 * NS, 240), "FB", "CC", 256 * NS, 3840, (("CB", 0, 128), ("Tt", 0, 240 - 16 * NS)))
        sgath(len(pairs) - 1)
        ssign(len(pairs) - 2)
        ssign(len(pairs) - 1)
        h = hlist("Pb", "Nb", "offb", 0, 240)
        h[0]()
        h[1]()

        bv(0, 4)
        fold(("pc", 0, 16 * NS), "FhB", "CC", 0, 256 * NS, (("CB", 0, 128), ("Th", 0, 16 * NS)))
        bv(4, 8)
        sgn(4, 8)
        cnta(4, 8)
        sgn(0, 4)
        cnta(0, 4)
        act(("pcS", 0, 240), ("pc", 0, 240), AF.Copy)
        bv(8, 12)
        bv(12, 15)
        tt(("mm", 16, 256), ("pa", 0, 240), ("pcS", 0, 240), A.min)
        tt(("Rg", 0, 256), (("mm", 0, 256), ("p2", 0, 16)), ("Rk", 0, 256), A.min)

        tt(("y", 16, 256), ("pb", 0, 240), ("SB", 0, 240), A.mult)
        tt(("x", 0, 256), (("y", 0, 256), ("p2", 0, 16)), ("Rg", 0, 256), A.min)
        op("v", lambda e: e.tensor_tensor_scan(T.Sc[:, :], T.RS[:, :], T.x[:, :], 0.0, A.mult, A.max),
           [("RS", 0, 256), ("x", 0, 256)], [("Sc", 0, 256)])
        sv = ("Sc", 15, 256, 16)
        ts(("Oj", 0, 16), sv, -1024.0, A.add, 1.0 / 2048, A.mult)
        ts(("Ni", 0, 16), sv, 863.5, A.add)
        cp(("ou", 0, 16), ("Oj", 0, 16))
        ts(("LH", 0, 16), ("Ni", 0, 16), 7, A.bitwise_and)
        ts(("LH", 16, 32), ("Ni", 0, 16), 3, A.logical_shift_right, 255, A.bitwise_and)
        cp((zn, 256, 512), (("ZK", 0, 4096), ("ou", 0, 16)))
        cp((zn, 512, 544), ("LH", 0, 32))

        dst = target(cores, rank, t)
        via = route(topo, core, dst)
        to = dst if via == core else via
        m, n = engines(topo, core, to)
        rid, pid = topo.addr(to, core)
        land, sem = (("L%d" % t), "arr%d" % t) if to == dst else (("R%d" % t), "rl%d" % t)
        before("g", [(zn, 256, 544)], [])
        g.remote_dma(T[land][:, :], T[zn][:, 256:544], T.sem[sem], T.sem["loc%d" % t], pid, rid, m)
        after("g", [(zn, 256, 544)], [], ("loc%d" % t, n))
        total["loc%d" % t] = n
        frm = cores[(rank - 1 - t % 3) % len(cores)]
        lc = "L%d" % t
        narr = engines(topo, route(topo, frm, core), core)[1]
        acc[lc] = [(0, PAY, True, ("arr%d" % t, narr), "net")]

        last = t == RO - 1
        if last:
            dma("y", "yz", T.yz[:, :], T[zn][:, 256:512], [(zn, 256, 512)], [])
        else:
            usum("pu", 0, 16, zn, 256, 512)
            z4((zn, 256, 512))
        if t == 0:
            consts2()
        ts(("NB", 0, 16), sv, 524288.0, A.is_lt, 67108864.0, A.mult)
        if not last:
            ts(("fl", 0, 16), sv, 524288.0, A.is_ge)
            op("p", lambda e: e.matmul(T.pu[:, 96:112], T.ON[:, 0:128], T.fl[:, :], True, True),
               [("ON", 0, 128), ("fl", 0, 16)], [("pu", 96, 112)])
        tt(("S3", 0, 16), sv, ("NB", 0, 16), A.add)
        tt(("keep", 0, 240), (("S3", 0, 16), ("cl", 0, 15)), ("TH", 16, 256), A.is_lt)
        if not last:
            ts(("vi", 0, 16), ("pu", 0, 16), FLOOR, A.add)
        tt(("kd", 0, 240), ("keep", 0, 240), ("d2", 0, 240), A.mult)
        if not last:
            tt(("v", 0, 16), ("pu", 0, 16), ("vi", 0, 16), A.subtract)
        tt((en, 16, 256), ("kd", 0, 240), ("d2", 256, 496), A.add)
        if not last:
            op("s", lambda e: e.activation(T.jk[:, :], T.pu[:, 96:112], AF.Identity, accum_out=T.As[:, :]), [("pu", 96, 112)],
               [("jk", 0, 16), ("As", 0, 1)])
            tt(("P", 16, 256), (("v", 0, 16), ("cl", 0, 15)), (en, 16, 256), A.mult)
            cp(("Ai", 0, 1), ("As", 0, 1))
            h = hlist("P", "N", "off", 16, 256)
            h[0]()
            ts(("Aj", 0, 1), ("Ai", 0, 1), 1, A.bitwise_and)
            h[1]()
            cp(("PT", 0, 1), ("Aj", 0, 1))
            act(("PT", 1, 2), ("PT", 0, 1), AF.Identity, 7.5)
            act(("PT", 2, 3), ("PT", 0, 1), AF.Identity, -0.5)
            tcol()
            shift(en, 2, 16)
            codes()
        else:
            cp(("X", 0, 512), ((en, 0, 256), ("l3", 0, 32)))

        tt(("ci", 0, 16), (lc, 256, 272), ("cb", 0, 16), A.add)
        ts(("e15", 0, 16), (lc, 272, 288), 8.0, A.mult, 1184.0, A.add)
        cp(("cu", 0, 16), ("ci", 0, 16))
        tt(("e16", 0, 16), ("e15", 0, 16), (lc, 256, 272), A.add)
        tt(("su", 0, 256), (DALL, ("cu", 0, 16)), (lc, 0, 256), A.add)
        ts((en, 0, 16), ("e16", 0, 16), 2048.0, A.mult)
        ts(("sh", 0, 256), ("su", 0, 256), 1, A.logical_shift_right)
        if not last:
            tt(("P", 0, 16), ("v", 0, 16), (en, 0, 16), A.mult)
        cp((DALL, ("cu", 0, 16)), ("sh", 0, 256))
        if not last:
            h = hlist("P", "N", "off", 0, 16)
            h[0]()
            shift(en, 1, 2)
            late = [h[1], lambda: tt(("Rk", 1, 256, 16), ("N", 0, 16), ("KC", 1, 256, 16), A.add)]
            continue

        dma("y", "yda", T.yd[:, 864:2048], T.D[:, 0:1184], [("D", 0, 1184)], [])
        dma("s", "ydb", T.yd[:, 0:864], T.D[:, 1184:2048], [("D", 1184, 2048)], [])
        cp(("X", 15, 512, 32), (en, 0, 16))
        cp(("X", 31, 512, 32), (en, 0, 16))
        op("v", lambda e: e.transpose(T.XT[:, :], T.X[:, :]), [("X", 0, 512)], [("XT", 0, 512)])
        ts(("YL", 0, 256), (("XT", 0, 512), ("l4", 0, 16)), 1.0 / 2048, A.mult, -1184.0, A.add)
        dma("y", "ye", T.ye[:, :], T.YL[:, :], [("YL", 0, 256)], [])

    for s in sorted(total):
        wait("g", (s, total[s]))
